import numpy as np
import ml_dtypes


def mxq(x, axis, fmt="e4m3"):
    dtype, down = {"e4m3": (ml_dtypes.float8_e4m3fn, 7), "e5m2": (ml_dtypes.float8_e5m2, 14)}[fmt]
    v = np.moveaxis(np.asarray(x, np.float32).astype(ml_dtypes.bfloat16).astype(np.float64), axis, -1)
    blocks = v.reshape(v.shape[:-1] + (-1, 32))
    amax = np.abs(blocks).max(-1, keepdims=True)
    byte = np.maximum(np.where(amax > 0, np.frexp(amax)[1] - 1 + 127, 0) - down, 1)
    scale = np.exp2(byte - 127.0)
    codes = (blocks / scale).astype(np.float32).astype(dtype).astype(np.float64)
    return np.moveaxis((codes * scale).reshape(v.shape), -1, axis)


WIDE = False


def mx_kscale(k):
    if not WIDE:
        return np.ones(k)
    levels = np.array([10, -10, 5, -5, 0])
    if k % 512:
        return np.exp2(np.random.permutation(np.resize(levels, k // 32))).repeat(32)
    a = np.empty((k // 512, 16))
    for p in range(k // 512):
        a[p, :8] = np.random.permutation(np.resize(levels, 8))
        for g in range(8):
            far = levels[np.abs(levels - a[p, g]) >= 10]
            a[p, g + 8] = far[np.random.randint(len(far))]
    return np.exp2(a.ravel()).repeat(32)


def f64(x):
    return np.asarray(x).astype(np.float64)


def striped(idx):
    return np.tile(idx.reshape(-1, 16).T, (8, 1)).astype(np.uint16)


def unstriped(offs):
    return offs[:16].T.reshape(-1).astype(np.int64)


def pack_weight(w):
    k, n = w.shape
    w = f64(np.asarray(w, np.float32).astype(ml_dtypes.bfloat16)).reshape(k // 32, 32, n)
    amax = np.abs(w).max(1)
    byte = np.clip(np.where(amax > 0, np.frexp(amax)[1] - 1 + 127 - 7, 1), 1, 254)
    scaled = (w * np.exp2(127.0 - byte)[:, None, :]).reshape(k, n).astype(np.float32)
    words = np.ascontiguousarray(scaled.reshape(k // 512, 128, 4, n).transpose(0, 1, 3, 2)).astype(ml_dtypes.float8_e4m3fn).view(np.uint8)
    return words, np.ascontiguousarray(byte.astype(np.uint8).reshape(k // 512, 16, n))


def unpack_weight(words, scales):
    g, p, n, _ = words.shape
    vals = np.ascontiguousarray(words).view(ml_dtypes.float8_e4m3fn).astype(np.float64) * np.repeat(np.exp2(scales.astype(np.float64) - 127.0), 8, axis=1)[..., None]
    return vals.transpose(0, 1, 3, 2).reshape(g * 512, n)


E2M1 = np.array([0.0, 0.5, 1.0, 1.5, 2.0, 3.0, 4.0, 6.0, -0.0, -0.5, -1.0, -1.5, -2.0, -3.0, -4.0, -6.0])


def pack_fp4(w):
    k, n = w.shape
    w = f64(np.asarray(w, np.float32).astype(ml_dtypes.bfloat16)).reshape(k // 32, 32, n)
    amax = np.abs(w).max(1)
    mant, ex = np.frexp(amax / 6.0)
    byte = np.clip(np.where(amax > 0, np.where(mant > 0.5, ex, ex - 1) + 127, 1), 1, 254)
    scaled = (w * np.exp2(127.0 - byte)[:, None, :]).reshape(k, n).astype(np.float32)
    c = np.ascontiguousarray(scaled.reshape(k // 512, 128, 4, n).transpose(0, 1, 3, 2)).astype(ml_dtypes.float4_e2m1fn).view(np.uint8) & 0xF
    words = (c[..., 0::2] | (c[..., 1::2] << 4)).reshape(k // 512, 128, 2 * n)
    return np.ascontiguousarray(words), np.ascontiguousarray(byte.astype(np.uint8).reshape(k // 512, 16, n))


def unpack_fp4(words, scales):
    g, _, n = scales.shape
    words = np.ascontiguousarray(words).reshape(g, 128, n, 2)
    nib = np.empty((g, 128, n, 4), np.uint8)
    nib[..., 0::2] = words & 0xF
    nib[..., 1::2] = words >> 4
    vals = E2M1[nib] * np.repeat(np.exp2(scales.astype(np.float64) - 127.0), 8, axis=1)[..., None]
    return vals.transpose(0, 1, 3, 2).reshape(g * 512, n)


def gelu(v):
    return 0.5 * v * (1.0 + np.tanh(np.sqrt(2.0 / np.pi) * (v + 0.044715 * v**3)))


K, T, S, H, N = 512, 2048, 1024, 512, 256


def setup_inputs():
    n = np.random.standard_normal
    s = mx_kscale(K)[:, None]
    u = mx_kscale(H)
    packed_xT = pack_weight(n((K, T)) * s)
    packed_w1 = pack_fp4(n((K, N)) / np.sqrt(2 * K) / s)
    packed_w3 = pack_fp4(n((H, N)) / np.sqrt(2 * H) / u[:, None])
    return {
        "x_words": packed_xT[0],
        "x_scales": packed_xT[1],
        "w1_words": packed_w1[0],
        "w1_scales": packed_w1[1],
        "w2": (n((K, H)) / np.sqrt(K) / s * u).astype(np.float32),
        "w3_words": packed_w3[0],
        "w3_scales": packed_w3[1],
        "offs": striped(np.random.permutation(T)[:S]),
    }


def reference(x_words, x_scales, w1_words, w1_scales, w2, w3_words, w3_scales, offs):
    xq = unpack_weight(x_words, x_scales)[:, unstriped(offs)]
    h = gelu(mxq(f64(w2), 0, "e4m3").T @ xq)
    return unpack_fp4(w1_words, w1_scales).T @ xq + unpack_fp4(w3_words, w3_scales).T @ mxq(h, 0, "e4m3")

@@ -1,0 +1,176 @@
+from contextlib import ExitStack
+
+import concourse.mybir as mybir
+
+K, T, S, H, N = 512, 2048, 1024, 512, 256
+FLOPS = 2 * K * H * S + 2 * K * N * S + 2 * H * N * S
+
+F32 = mybir.dt.float32
+BF16 = mybir.dt.bfloat16
+I32 = mybir.dt.int32
+U32 = mybir.dt.uint32
+U16 = mybir.dt.uint16
+U8 = mybir.dt.uint8
+FP8X4 = mybir.dt.float8_e4m3fn_x4
+FP4X4 = mybir.dt.float4_e2m1fn_x4
+GELU = mybir.ActivationFunctionType.Gelu_apprx_tanh
+
+P = 128
+PACK = 4
+CHUNK = 128
+HALF = 512
+
+
+def load_scale_rows(queue, plane, rows):
+    for r in range(4):
+        queue.dma_start(out=plane[r:P:32, :].bitcast(I32), in_=rows[r:16:4, :].bitcast(I32))
+
+
+def tile_picked_lora_gelu_p_kernel(
+    tc, x_words, x_scales, w1_words, w1_scales, w2, w3_words, w3_scales, offs, out
+):
+    nc = tc.nc
+    with ExitStack() as ctx:
+        keep = ctx.enter_context(tc.tile_pool(name="keep", bufs=1))
+        psum = ctx.enter_context(tc.psum_pool(name="psum", bufs=1))
+
+        offsets = keep.tile([P, S // 16], U16, name="offsets")
+        xs_table = keep.tile([P, T], U8, name="xs_table", tag="slot_xs", align_bytes=64)
+        xw_table = keep.tile([P, T], I32, name="xw_table", align_bytes=64)
+        w1_codes = keep.tile([P, 2 * N], U8, name="w1_codes", align_bytes=64)
+        w3_codes = keep.tile([P, 2 * N], U8, name="w3_codes", align_bytes=64)
+        w1_plane = keep.tile([P, N], U8, name="w1_plane", align_bytes=64)
+        warm_in = keep.tile([P, 1], F32, name="warm_in", tag="slot_w2", align_bytes=64)
+        warm_out = keep.tile([P, 1], F32, name="warm_out", tag="slot_w3", align_bytes=64)
+
+        nc.vector.memset(xs_table[:].bitcast(I32), 0)
+        nc.vector.memset(w1_plane[:].bitcast(I32), 0)
+        nc.gpsimd.memset(warm_in[:], 0.0)
+
+        nc.sync.dma_start(offsets[:], offs)
+        load_scale_rows(nc.sync, xs_table, x_scales[0])
+        nc.scalar.dma_start(out=xw_table[:], in_=x_words[0].rearrange("p n t -> p (n t)").bitcast(I32))
+        nc.scalar.dma_start(out=w1_codes[:].bitcast(I32), in_=w1_words[0].bitcast(I32))
+        nc.gpsimd.dma_start(out=w3_codes[:].bitcast(I32), in_=w3_words[0].bitcast(I32))
+        nc.scalar.activation(out=warm_out[:], in_=warm_in[:], func=GELU)
+        w2_raw = keep.tile([P, PACK, H], F32, name="w2_raw", tag="slot_w2", align_bytes=64)
+        nc.sync.dma_start(out=w2_raw[:], in_=w2.rearrange("(p j) c -> p j c", j=PACK))
+        load_scale_rows(nc.scalar, w1_plane, w1_scales[0])
+        w3_plane = keep.tile([P, N], U8, name="w3_plane", tag="slot_w3", align_bytes=64)
+        nc.gpsimd.memset(w3_plane[:].bitcast(I32), 0)
+        load_scale_rows(nc.sync, w3_plane, w3_scales[0])
+
+        x_plane = keep.tile([P, S], U8, name="x_plane", align_bytes=64)
+        nc.vector.tensor_copy(x_plane[:], xs_table[:].indirect(offsets[:]))
+        x_codes = []
+
+        def gather_words(a, tag):
+            codes = keep.tile([P, HALF], U32, name=f"x_codes{a}", tag=tag, align_bytes=64)
+            nc.vector.tensor_copy(codes[:], xw_table[:].bitcast(U32).indirect(offsets[:, a * 32 : (a + 1) * 32]))
+            x_codes.append(codes)
+
+        gather_words(0, "slot_xs")
+
+        def x_operand(lo, width):
+            a, c = divmod(lo, HALF)
+            return x_codes[a][:, c : c + width].bitcast(FP8X4), x_plane[:, lo : lo + width]
+
+        def weight_pass(dst, codes, plane, m, rhs, start, stop):
+            nc.tensor.matmul_mx(
+                out=dst,
+                lhsT=codes[:, 2 * P * m : 2 * P * (m + 1)].bitcast(FP4X4),
+                lhsT_scale=plane[:, P * m : P * (m + 1)],
+                rhs=rhs[0],
+                rhs_scale=rhs[1],
+                start=start,
+                stop=stop,
+            )
+
+        wide = [psum.tile([P, HALF], F32, name=f"wide{m}", tag=f"wide{m}") for m in range(2)]
+        for m in range(2):
+            weight_pass(wide[m][:], w1_codes, w1_plane, m, x_operand(0, HALF), True, False)
+
+        w2_codes = keep.tile([P, PACK * P], U32, name="w2_codes", align_bytes=64)
+        w2_plane = keep.tile([P, PACK * P], U8, name="w2_plane", align_bytes=64)
+        SCALAR_SHARE = 44
+        grouped = keep.tile([P, PACK, P, PACK], BF16, name="w2_grouped", tag="slot_grouped", align_bytes=64)
+        src = w2_raw[:].rearrange("p j (m t) -> p m j t", t=PACK)
+        dst = grouped[:].rearrange("p t m j -> p m j t")
+        nc.scalar.copy(out=dst[:, :SCALAR_SHARE], in_=src[:, :SCALAR_SHARE])
+        nc.vector.tensor_copy(out=dst[:, SCALAR_SHARE:], in_=src[:, SCALAR_SHARE:])
+        for t in range(PACK):
+            nc.vector.quantize_mx(
+                out=w2_codes[:, t * P : (t + 1) * P].bitcast(FP8X4),
+                scales=w2_plane[:, t * P : (t + 1) * P],
+                in_=grouped[:, t].rearrange("p m j -> p (m j)"),
+            )
+
+        gather_words(1, "slot_grouped")
+
+        h_vals = keep.tile([P, S * PACK], BF16, name="h_vals", align_bytes=64)
+        h_codes = keep.tile([P, S], U32, name="h_codes", align_bytes=64)
+        h_plane = keep.tile([P, S], U8, name="h_plane", align_bytes=64)
+
+        def hidden(c):
+            bank = psum.tile([P, PACK, CHUNK], F32, name=f"hbank{c}", tag=f"hbank{c % 4}")
+            rhs = x_operand(c * CHUNK, CHUNK)
+            for t in range(PACK):
+                nc.tensor.matmul_mx(
+                    out=bank[:, t, :],
+                    lhsT=w2_codes[:, t * P : (t + 1) * P].bitcast(FP8X4),
+                    lhsT_scale=w2_plane[:, t * P : (t + 1) * P],
+                    rhs=rhs[0],
+                    rhs_scale=rhs[1],
+                    start=True,
+                    stop=True,
+                )
+            dst = h_vals[:, c * CHUNK * PACK : (c + 1) * CHUNK * PACK].rearrange("p (n t) -> p n t", t=PACK)
+            nc.scalar.activation(out=dst, in_=bank[:].rearrange("p t n -> p n t"), func=GELU)
+
+        def quantise_h(lo, width):
+            nc.vector.quantize_mx(
+                out=h_codes[:, lo : lo + width].bitcast(FP8X4),
+                scales=h_plane[:, lo : lo + width],
+                in_=h_vals[:, lo * PACK : (lo + width) * PACK],
+            )
+
+        def h_operand(lo, width):
+            return h_codes[:, lo : lo + width].bitcast(FP8X4), h_plane[:, lo : lo + width]
+
+        out_rows = out.rearrange("(m p) s -> p m s", p=P)
+
+        def finish_wide():
+            for m in range(2):
+                weight_pass(wide[m][:], w3_codes, w3_plane, m, h_operand(0, HALF), False, True)
+            for m in range(2):
+                staged = keep.tile([P, HALF], F32, name=f"staged_wide{m}")
+                nc.vector.tensor_copy(out=staged[:], in_=wide[m][:])
+                nc.sync.dma_start(out=out_rows[:, m, 0:HALF], in_=staged[:])
+
+        def finish_chunk(c, tags):
+            lo = c * CHUNK
+            staged = keep.tile([P, 2, CHUNK], F32, name=f"staged{c}")
+            if len(tags) == 1:
+                bank = psum.tile([P, 2, CHUNK], F32, name=f"obank{c}", tag=tags[0])
+                for m in range(2):
+                    weight_pass(bank[:, m, :], w1_codes, w1_plane, m, x_operand(lo, CHUNK), True, False)
+                    weight_pass(bank[:, m, :], w3_codes, w3_plane, m, h_operand(lo, CHUNK), False, True)
+                nc.vector.tensor_copy(out=staged[:], in_=bank[:])
+            else:
+                banks = [psum.tile([P, CHUNK], F32, name=f"obank{c}_{m}", tag=tags[m]) for m in range(2)]
+                for m in range(2):
+                    weight_pass(banks[m][:], w1_codes, w1_plane, m, x_operand(lo, CHUNK), True, False)
+                for m in range(2):
+                    weight_pass(banks[m][:], w3_codes, w3_plane, m, h_operand(lo, CHUNK), False, True)
+                nc.vector.tensor_copy(out=staged[:, 0, :], in_=banks[0][:])
+                nc.scalar.copy(out=staged[:, 1, :], in_=banks[1][:])
+            nc.sync.dma_start(out=out_rows[:, :, lo : lo + CHUNK], in_=staged[:])
+
+        for c in range(8):
+            hidden(c)
+            if c == 1 or c == 3:
+                quantise_h((c - 1) * CHUNK, 2 * CHUNK)
+        finish_wide()
+        for c, tags in ((4, ["narrow0"]), (5, ["narrow1"]), (6, ["hbank0"]), (7, ["hbank1", "hbank2"])):
+            quantise_h(c * CHUNK, CHUNK)
+            finish_chunk(c, tags)

@@ -21,9 +21,9 @@ CHUNK = 128
 HALF = 512
 
 
-def load_scale_rows(queue, plane, rows):
+def load_scale_rows(queues, plane, rows):
     for r in range(4):
-        queue.dma_start(out=plane[r:P:32, :].bitcast(I32), in_=rows[r:16:4, :].bitcast(I32))
+        queues[r % len(queues)].dma_start(out=plane[r:P:32, :].bitcast(I32), in_=rows[r:16:4, :].bitcast(I32))
 
 
 def tile_picked_lora_gelu_p_kernel(
@@ -35,44 +35,41 @@ def tile_picked_lora_gelu_p_kernel(
         psum = ctx.enter_context(tc.psum_pool(name="psum", bufs=1))
 
         offsets = keep.tile([P, S // 16], U16, name="offsets")
-        xs_table = keep.tile([P, T], U8, name="xs_table", tag="slot_xs", align_bytes=64)
+        xs_table = keep.tile([P, T], U8, name="xs_table", align_bytes=64)
         xw_table = keep.tile([P, T], I32, name="xw_table", align_bytes=64)
+        warm = keep.tile([P, 16], F32, name="warm")
+        w2_raw = keep.tile([P, PACK, H], F32, name="w2_raw", align_bytes=64)
         w1_codes = keep.tile([P, 2 * N], U8, name="w1_codes", align_bytes=64)
         w3_codes = keep.tile([P, 2 * N], U8, name="w3_codes", align_bytes=64)
         w1_plane = keep.tile([P, N], U8, name="w1_plane", align_bytes=64)
-        warm_in = keep.tile([P, 1], F32, name="warm_in", tag="slot_w2", align_bytes=64)
-        warm_out = keep.tile([P, 1], F32, name="warm_out", tag="slot_w3", align_bytes=64)
+        w3_plane = keep.tile([P, N], U8, name="w3_plane", align_bytes=64)
 
         nc.vector.memset(xs_table[:].bitcast(I32), 0)
+        nc.vector.memset(warm[:, 0:1], 0.0)
         nc.vector.memset(w1_plane[:].bitcast(I32), 0)
-        nc.gpsimd.memset(warm_in[:], 0.0)
+        nc.gpsimd.memset(w3_plane[:].bitcast(I32), 0)
 
         nc.sync.dma_start(offsets[:], offs)
-        load_scale_rows(nc.sync, xs_table, x_scales[0])
-        nc.scalar.dma_start(out=xw_table[:], in_=x_words[0].rearrange("p n t -> p (n t)").bitcast(I32))
-        nc.scalar.dma_start(out=w1_codes[:].bitcast(I32), in_=w1_words[0].bitcast(I32))
-        nc.gpsimd.dma_start(out=w3_codes[:].bitcast(I32), in_=w3_words[0].bitcast(I32))
-        nc.scalar.activation(out=warm_out[:], in_=warm_in[:], func=GELU)
-        w2_raw = keep.tile([P, PACK, H], F32, name="w2_raw", tag="slot_w2", align_bytes=64)
+        nc.sync.dma_start(out=w1_codes[:].bitcast(I32), in_=w1_words[0].bitcast(I32))
+        nc.sync.dma_start(out=w3_codes[:].bitcast(I32), in_=w3_words[0].bitcast(I32))
+        load_scale_rows([nc.sync, nc.scalar], xs_table, x_scales[0])
         nc.sync.dma_start(out=w2_raw[:], in_=w2.rearrange("(p j) c -> p j c", j=PACK))
-        load_scale_rows(nc.scalar, w1_plane, w1_scales[0])
-        w3_plane = keep.tile([P, N], U8, name="w3_plane", tag="slot_w3", align_bytes=64)
-        nc.gpsimd.memset(w3_plane[:].bitcast(I32), 0)
-        load_scale_rows(nc.sync, w3_plane, w3_scales[0])
+        nc.sync.dma_start(out=xw_table[:], in_=x_words[0].rearrange("p n t -> p (n t)").bitcast(I32))
+        nc.scalar.activation(out=warm[:, 8:9], in_=warm[:, 0:1], func=GELU)
+        load_scale_rows([nc.scalar], w1_plane, w1_scales[0])
+        load_scale_rows([nc.gpsimd], w3_plane, w3_scales[0])
 
         x_plane = keep.tile([P, S], U8, name="x_plane", align_bytes=64)
         nc.vector.tensor_copy(x_plane[:], xs_table[:].indirect(offsets[:]))
         x_codes = []
 
         def gather_words(a, tag):
-            codes = keep.tile([P, HALF], U32, name=f"x_codes{a}", tag=tag, align_bytes=64)
-            nc.vector.tensor_copy(codes[:], xw_table[:].bitcast(U32).indirect(offsets[:, a * 32 : (a + 1) * 32]))
+            codes = keep.tile([P, 256], U32, name=f"x_codes{a}", tag=tag, align_bytes=64)
+            nc.vector.tensor_copy(codes[:], xw_table[:].bitcast(U32).indirect(offsets[:, a * 16 : (a + 1) * 16]))
             x_codes.append(codes)
 
-        gather_words(0, "slot_xs")
-
         def x_operand(lo, width):
-            a, c = divmod(lo, HALF)
+            a, c = divmod(lo, 256)
             return x_codes[a][:, c : c + width].bitcast(FP8X4), x_plane[:, lo : lo + width]
 
         def weight_pass(dst, codes, plane, m, rhs, start, stop):
@@ -86,14 +83,10 @@ def tile_picked_lora_gelu_p_kernel(
                 stop=stop,
             )
 
-        wide = [psum.tile([P, HALF], F32, name=f"wide{m}", tag=f"wide{m}") for m in range(2)]
-        for m in range(2):
-            weight_pass(wide[m][:], w1_codes, w1_plane, m, x_operand(0, HALF), True, False)
-
         w2_codes = keep.tile([P, PACK * P], U32, name="w2_codes", align_bytes=64)
         w2_plane = keep.tile([P, PACK * P], U8, name="w2_plane", align_bytes=64)
         SCALAR_SHARE = 44
-        grouped = keep.tile([P, PACK, P, PACK], BF16, name="w2_grouped", tag="slot_grouped", align_bytes=64)
+        grouped = keep.tile([P, PACK, P, PACK], BF16, name="w2_grouped", align_bytes=64)
         src = w2_raw[:].rearrange("p j (m t) -> p m j t", t=PACK)
         dst = grouped[:].rearrange("p t m j -> p m j t")
         nc.scalar.copy(out=dst[:, :SCALAR_SHARE], in_=src[:, :SCALAR_SHARE])
@@ -105,14 +98,22 @@ def tile_picked_lora_gelu_p_kernel(
                 in_=grouped[:, t].rearrange("p m j -> p (m j)"),
             )
 
-        gather_words(1, "slot_grouped")
+        warm_bank = psum.tile([P, PACK, P], F32, name="warm_bank", tag="obank4")
+        for i in range(6):
+            codes, plane = w2_codes[:, 0:P].bitcast(FP8X4), w2_plane[:, 0:P]
+            nc.tensor.matmul_mx(
+                out=warm_bank[:, i % PACK, :], lhsT=codes, lhsT_scale=plane, rhs=codes, rhs_scale=plane, start=True, stop=True
+            )
+
+        for a in range(4):
+            gather_words(a, f"slot_codes{a}")
 
         h_vals = keep.tile([P, S * PACK], BF16, name="h_vals", align_bytes=64)
         h_codes = keep.tile([P, S], U32, name="h_codes", align_bytes=64)
         h_plane = keep.tile([P, S], U8, name="h_plane", align_bytes=64)
 
         def hidden(c):
-            bank = psum.tile([P, PACK, CHUNK], F32, name=f"hbank{c}", tag=f"hbank{c % 4}")
+            bank = psum.tile([P, PACK, CHUNK], F32, name=f"hbank{c}", tag=f"hbank{c % 3}")
             rhs = x_operand(c * CHUNK, CHUNK)
             for t in range(PACK):
                 nc.tensor.matmul_mx(
@@ -139,38 +140,34 @@ def tile_picked_lora_gelu_p_kernel(
 
         out_rows = out.rearrange("(m p) s -> p m s", p=P)
 
-        def finish_wide():
-            for m in range(2):
-                weight_pass(wide[m][:], w3_codes, w3_plane, m, h_operand(0, HALF), False, True)
-            for m in range(2):
-                staged = keep.tile([P, HALF], F32, name=f"staged_wide{m}")
-                nc.vector.tensor_copy(out=staged[:], in_=wide[m][:])
-                nc.sync.dma_start(out=out_rows[:, m, 0:HALF], in_=staged[:])
-
-        def finish_chunk(c, tags):
+        def finish_chunk(c, staged):
             lo = c * CHUNK
-            staged = keep.tile([P, 2, CHUNK], F32, name=f"staged{c}")
-            if len(tags) == 1:
-                bank = psum.tile([P, 2, CHUNK], F32, name=f"obank{c}", tag=tags[0])
+            if c < 7:
+                bank = psum.tile([P, 2, CHUNK], F32, name=f"obank{c}", tag=f"obank{c % 5}")
                 for m in range(2):
                     weight_pass(bank[:, m, :], w1_codes, w1_plane, m, x_operand(lo, CHUNK), True, False)
                     weight_pass(bank[:, m, :], w3_codes, w3_plane, m, h_operand(lo, CHUNK), False, True)
-                nc.vector.tensor_copy(out=staged[:], in_=bank[:])
+                if c < 5:
+                    nc.vector.tensor_copy(out=staged, in_=bank[:])
+                else:
+                    nc.scalar.copy(out=staged, in_=bank[:])
             else:
-                banks = [psum.tile([P, CHUNK], F32, name=f"obank{c}_{m}", tag=tags[m]) for m in range(2)]
+                banks = [psum.tile([P, CHUNK], F32, name=f"obank{c}_{m}", tag=f"obank{(c + m) % 5}") for m in range(2)]
                 for m in range(2):
                     weight_pass(banks[m][:], w1_codes, w1_plane, m, x_operand(lo, CHUNK), True, False)
                 for m in range(2):
                     weight_pass(banks[m][:], w3_codes, w3_plane, m, h_operand(lo, CHUNK), False, True)
                 nc.vector.tensor_copy(out=staged[:, 0, :], in_=banks[0][:])
                 nc.scalar.copy(out=staged[:, 1, :], in_=banks[1][:])
-            nc.sync.dma_start(out=out_rows[:, :, lo : lo + CHUNK], in_=staged[:])
 
-        for c in range(8):
+        for c in range(3):
             hidden(c)
-            if c == 1 or c == 3:
-                quantise_h((c - 1) * CHUNK, 2 * CHUNK)
-        finish_wide()
-        for c, tags in ((4, ["narrow0"]), (5, ["narrow1"]), (6, ["hbank0"]), (7, ["hbank1", "hbank2"])):
-            quantise_h(c * CHUNK, CHUNK)
-            finish_chunk(c, tags)
+        for first, count in ((0, 2), (2, 2), (4, 2), (6, 1), (7, 1)):
+            staged = keep.tile([P, 2, count * CHUNK], F32, name=f"staged{first}")
+            for i in range(count):
+                c = first + i
+                quantise_h(c * CHUNK, CHUNK)
+                if c + 3 < 8:
+                    hidden(c + 3)
+                finish_chunk(c, staged[:, :, i * CHUNK : (i + 1) * CHUNK])
+            nc.sync.dma_start(out=out_rows[:, :, first * CHUNK : (first + count) * CHUNK], in_=staged[:])

@@ -18,7 +18,9 @@ GELU = mybir.ActivationFunctionType.Gelu_apprx_tanh
 P = 128
 PACK = 4
 CHUNK = 128
-HALF = 512
+SCALAR_SHARE = 52
+WARM_PASSES = 4
+WARM_WIDTH = 256
 
 
 def load_scale_rows(queues, plane, rows):
@@ -38,39 +40,67 @@ def tile_picked_lora_gelu_p_kernel(
         xs_table = keep.tile([P, T], U8, name="xs_table", align_bytes=64)
         xw_table = keep.tile([P, T], I32, name="xw_table", align_bytes=64)
         warm = keep.tile([P, 16], F32, name="warm")
-        w2_raw = keep.tile([P, PACK, H], F32, name="w2_raw", align_bytes=64)
-        w1_codes = keep.tile([P, 2 * N], U8, name="w1_codes", align_bytes=64)
-        w3_codes = keep.tile([P, 2 * N], U8, name="w3_codes", align_bytes=64)
+        w2_raw = keep.tile([P, PACK, H], F32, name="w2_raw", tag="raw", align_bytes=64)
         w1_plane = keep.tile([P, N], U8, name="w1_plane", align_bytes=64)
-        w3_plane = keep.tile([P, N], U8, name="w3_plane", align_bytes=64)
+        x_plane = keep.tile([P, S], U8, name="x_plane", align_bytes=64)
 
         nc.vector.memset(xs_table[:].bitcast(I32), 0)
         nc.vector.memset(warm[:, 0:1], 0.0)
         nc.vector.memset(w1_plane[:].bitcast(I32), 0)
+        nc.vector.memset(x_plane[:].bitcast(I32), 0)
+        w3_plane = keep.tile([P, N], U8, name="w3_plane", align_bytes=64)
         nc.gpsimd.memset(w3_plane[:].bitcast(I32), 0)
+        w1_codes = keep.tile([P, 2 * N], U8, name="w1_codes", align_bytes=64)
+        w3_codes = keep.tile([P, 2 * N], U8, name="w3_codes", align_bytes=64)
 
         nc.sync.dma_start(offsets[:], offs)
+        w2_rows = w2.rearrange("(p j) c -> p j c", j=PACK)
         nc.sync.dma_start(out=w1_codes[:].bitcast(I32), in_=w1_words[0].bitcast(I32))
         nc.sync.dma_start(out=w3_codes[:].bitcast(I32), in_=w3_words[0].bitcast(I32))
-        load_scale_rows([nc.sync, nc.scalar], xs_table, x_scales[0])
-        nc.sync.dma_start(out=w2_raw[:], in_=w2.rearrange("(p j) c -> p j c", j=PACK))
+        nc.sync.dma_start(out=xs_table[0:P:8, :].bitcast(I32), in_=x_scales[0].bitcast(I32))
+        nc.sync.dma_start(out=w2_raw[:], in_=w2_rows)
         nc.sync.dma_start(out=xw_table[:], in_=x_words[0].rearrange("p n t -> p (n t)").bitcast(I32))
         nc.scalar.activation(out=warm[:, 8:9], in_=warm[:, 0:1], func=GELU)
         load_scale_rows([nc.scalar], w1_plane, w1_scales[0])
         load_scale_rows([nc.gpsimd], w3_plane, w3_scales[0])
 
-        x_plane = keep.tile([P, S], U8, name="x_plane", align_bytes=64)
-        nc.vector.tensor_copy(x_plane[:], xs_table[:].indirect(offsets[:]))
-        x_codes = []
+        picked = keep.tile([P, S], U8, name="picked", align_bytes=64)
+        nc.vector.tensor_copy(picked[:], xs_table[:].indirect(offsets[:]))
+        for r in range(4):
+            nc.sync.dma_start(out=x_plane[r:P:32, :].bitcast(I32), in_=picked[8 * r : P : 32, :].bitcast(I32))
 
-        def gather_words(a, tag):
-            codes = keep.tile([P, 256], U32, name=f"x_codes{a}", tag=tag, align_bytes=64)
-            nc.vector.tensor_copy(codes[:], xw_table[:].bitcast(U32).indirect(offsets[:, a * 16 : (a + 1) * 16]))
-            x_codes.append(codes)
+        w2_codes = keep.tile([P, PACK * P], U32, name="w2_codes", align_bytes=64)
+        w2_plane = keep.tile([P, PACK * P], U8, name="w2_plane", align_bytes=64)
+        grouped = keep.tile([P, PACK, P, PACK], BF16, name="w2_grouped", align_bytes=64)
+        src = w2_raw[:].rearrange("p j (m t) -> p m j t", t=PACK)
+        dst = grouped[:].rearrange("p t m j -> p m j t")
+        nc.scalar.copy(out=dst[:, :SCALAR_SHARE], in_=src[:, :SCALAR_SHARE])
+        nc.vector.tensor_copy(out=dst[:, SCALAR_SHARE:], in_=src[:, SCALAR_SHARE:])
+        nc.vector.quantize_mx(
+            out=w2_codes[:].bitcast(FP8X4), scales=w2_plane[:], in_=grouped[:].rearrange("p t m j -> p (t m j)")
+        )
 
-        def x_operand(lo, width):
-            a, c = divmod(lo, 256)
-            return x_codes[a][:, c : c + width].bitcast(FP8X4), x_plane[:, lo : lo + width]
+        warm_bank = psum.tile([P, WARM_WIDTH], F32, name="warm_bank", tag="bank5")
+        for i in range(WARM_PASSES):
+            nc.tensor.matmul_mx(
+                out=warm_bank[:], lhsT=w2_codes[:, 0:P].bitcast(FP8X4), lhsT_scale=w2_plane[:, 0:P],
+                rhs=w2_codes[:, 0:WARM_WIDTH].bitcast(FP8X4), rhs_scale=w2_plane[:, 0:WARM_WIDTH], start=True, stop=True,
+            )
+
+
+        x_codes = {}
+
+        def gather_words(lo, width):
+            codes = keep.tile([P, width], U32, name=f"x_codes{lo}", align_bytes=64)
+            nc.vector.tensor_copy(codes[:], xw_table[:].bitcast(U32).indirect(offsets[:, lo // 16 : (lo + width) // 16]))
+            for c in range(0, width, CHUNK):
+                x_codes[(lo + c) // CHUNK] = codes[:, c : c + CHUNK]
+
+        for lo, width in ((0, 256), (256, 256), (512, 512)):
+            gather_words(lo, width)
+
+        def x_operand(c):
+            return x_codes[c].bitcast(FP8X4), x_plane[:, c * CHUNK : (c + 1) * CHUNK]
 
         def weight_pass(dst, codes, plane, m, rhs, start, stop):
             nc.tensor.matmul_mx(
@@ -83,38 +113,17 @@ def tile_picked_lora_gelu_p_kernel(
                 stop=stop,
             )
 
-        w2_codes = keep.tile([P, PACK * P], U32, name="w2_codes", align_bytes=64)
-        w2_plane = keep.tile([P, PACK * P], U8, name="w2_plane", align_bytes=64)
-        SCALAR_SHARE = 44
-        grouped = keep.tile([P, PACK, P, PACK], BF16, name="w2_grouped", align_bytes=64)
-        src = w2_raw[:].rearrange("p j (m t) -> p m j t", t=PACK)
-        dst = grouped[:].rearrange("p t m j -> p m j t")
-        nc.scalar.copy(out=dst[:, :SCALAR_SHARE], in_=src[:, :SCALAR_SHARE])
-        nc.vector.tensor_copy(out=dst[:, SCALAR_SHARE:], in_=src[:, SCALAR_SHARE:])
-        for t in range(PACK):
-            nc.vector.quantize_mx(
-                out=w2_codes[:, t * P : (t + 1) * P].bitcast(FP8X4),
-                scales=w2_plane[:, t * P : (t + 1) * P],
-                in_=grouped[:, t].rearrange("p m j -> p (m j)"),
-            )
-
-        warm_bank = psum.tile([P, PACK, P], F32, name="warm_bank", tag="obank4")
-        for i in range(6):
-            codes, plane = w2_codes[:, 0:P].bitcast(FP8X4), w2_plane[:, 0:P]
-            nc.tensor.matmul_mx(
-                out=warm_bank[:, i % PACK, :], lhsT=codes, lhsT_scale=plane, rhs=codes, rhs_scale=plane, start=True, stop=True
-            )
-
-        for a in range(4):
-            gather_words(a, f"slot_codes{a}")
-
-        h_vals = keep.tile([P, S * PACK], BF16, name="h_vals", align_bytes=64)
         h_codes = keep.tile([P, S], U32, name="h_codes", align_bytes=64)
         h_plane = keep.tile([P, S], U8, name="h_plane", align_bytes=64)
+        h_tiles = {}
+        for first, count in ((0, 2), (2, 2), (4, 1), (5, 1), (6, 1), (7, 1)):
+            tile = keep.tile([P, count * CHUNK * PACK], BF16, name=f"h_vals{first}", tag=f"slot{first}", align_bytes=64)
+            for i in range(count):
+                h_tiles[first + i] = (tile, i)
 
-        def hidden(c):
-            bank = psum.tile([P, PACK, CHUNK], F32, name=f"hbank{c}", tag=f"hbank{c % 3}")
-            rhs = x_operand(c * CHUNK, CHUNK)
+        def hidden(c, tag):
+            bank = psum.tile([P, PACK, CHUNK], F32, name=f"hbank{c}", tag=tag)
+            rhs = x_operand(c)
             for t in range(PACK):
                 nc.tensor.matmul_mx(
                     out=bank[:, t, :],
@@ -125,49 +134,85 @@ def tile_picked_lora_gelu_p_kernel(
                     start=True,
                     stop=True,
                 )
-            dst = h_vals[:, c * CHUNK * PACK : (c + 1) * CHUNK * PACK].rearrange("p (n t) -> p n t", t=PACK)
+            tile, i = h_tiles[c]
+            dst = tile[:, i * CHUNK * PACK : (i + 1) * CHUNK * PACK].rearrange("p (n t) -> p n t", t=PACK)
             nc.scalar.activation(out=dst, in_=bank[:].rearrange("p t n -> p n t"), func=GELU)
 
-        def quantise_h(lo, width):
+        def quantise_h(first, count):
+            lo, width = first * CHUNK, count * CHUNK
             nc.vector.quantize_mx(
                 out=h_codes[:, lo : lo + width].bitcast(FP8X4),
                 scales=h_plane[:, lo : lo + width],
-                in_=h_vals[:, lo * PACK : (lo + width) * PACK],
+                in_=h_tiles[first][0][:],
             )
 
-        def h_operand(lo, width):
-            return h_codes[:, lo : lo + width].bitcast(FP8X4), h_plane[:, lo : lo + width]
+        def h_operand(c):
+            return h_codes[:, c * CHUNK : (c + 1) * CHUNK].bitcast(FP8X4), h_plane[:, c * CHUNK : (c + 1) * CHUNK]
 
         out_rows = out.rearrange("(m p) s -> p m s", p=P)
+        banks = {}
 
-        def finish_chunk(c, staged):
-            lo = c * CHUNK
-            if c < 7:
-                bank = psum.tile([P, 2, CHUNK], F32, name=f"obank{c}", tag=f"obank{c % 5}")
-                for m in range(2):
-                    weight_pass(bank[:, m, :], w1_codes, w1_plane, m, x_operand(lo, CHUNK), True, False)
-                    weight_pass(bank[:, m, :], w3_codes, w3_plane, m, h_operand(lo, CHUNK), False, True)
-                if c < 5:
-                    nc.vector.tensor_copy(out=staged, in_=bank[:])
-                else:
-                    nc.scalar.copy(out=staged, in_=bank[:])
-            else:
-                banks = [psum.tile([P, CHUNK], F32, name=f"obank{c}_{m}", tag=f"obank{(c + m) % 5}") for m in range(2)]
-                for m in range(2):
-                    weight_pass(banks[m][:], w1_codes, w1_plane, m, x_operand(lo, CHUNK), True, False)
-                for m in range(2):
-                    weight_pass(banks[m][:], w3_codes, w3_plane, m, h_operand(lo, CHUNK), False, True)
-                nc.vector.tensor_copy(out=staged[:, 0, :], in_=banks[0][:])
-                nc.scalar.copy(out=staged[:, 1, :], in_=banks[1][:])
-
-        for c in range(3):
-            hidden(c)
-        for first, count in ((0, 2), (2, 2), (4, 2), (6, 1), (7, 1)):
-            staged = keep.tile([P, 2, count * CHUNK], F32, name=f"staged{first}")
+        def open_piece(ms, first, count, tag):
+            bank = psum.tile([P, len(ms), count * CHUNK], F32, name=f"obank_{first}_{ms[0]}", tag=tag)
+            banks[(first, ms[0])] = bank
             for i in range(count):
-                c = first + i
-                quantise_h(c * CHUNK, CHUNK)
-                if c + 3 < 8:
-                    hidden(c + 3)
-                finish_chunk(c, staged[:, :, i * CHUNK : (i + 1) * CHUNK])
+                for k, m in enumerate(ms):
+                    weight_pass(
+                        bank[:, k, i * CHUNK : (i + 1) * CHUNK], w1_codes, w1_plane, m,
+                        x_operand(first + i), i == 0 and k == 0, False,
+                    )
+
+        def add_hidden(ms, first, count, i):
+            bank = banks[(first, ms[0])]
+            for k, m in enumerate(ms):
+                weight_pass(
+                    bank[:, k, i * CHUNK : (i + 1) * CHUNK], w3_codes, w3_plane, m,
+                    h_operand(first + i), False, i == count - 1 and k == len(ms) - 1,
+                )
+
+        def store(first, count, staged):
             nc.sync.dma_start(out=out_rows[:, :, first * CHUNK : (first + count) * CHUNK], in_=staged[:])
+
+        def empty(first, count, tag, copy):
+            staged = keep.tile([P, 2, count * CHUNK], F32, name=f"staged{first}", tag=tag, align_bytes=64)
+            copy(out=staged[:], in_=banks[(first, 0)][:])
+            store(first, count, staged)
+
+        both = (0, 1)
+        for c in range(4):
+            hidden(c, f"bank{c}")
+        open_piece(both, 0, 2, "bank4")
+        hidden(4, "bank0")
+        quantise_h(0, 2)
+        add_hidden(both, 0, 2, 0)
+        add_hidden(both, 0, 2, 1)
+        hidden(5, "bank1")
+        empty(0, 2, "staged0", nc.vector.tensor_copy)
+        open_piece(both, 2, 2, "bank2")
+        hidden(6, "bank3")
+        quantise_h(2, 2)
+        add_hidden(both, 2, 2, 0)
+        add_hidden(both, 2, 2, 1)
+        hidden(7, "bank0")
+        quantise_h(4, 1)
+        open_piece(both, 4, 1, "bank4")
+        add_hidden(both, 4, 1, 0)
+        quantise_h(5, 1)
+        empty(2, 2, "slot5", nc.vector.tensor_copy)
+        open_piece(both, 5, 1, "bank1")
+        add_hidden(both, 5, 1, 0)
+        quantise_h(6, 1)
+        open_piece(both, 6, 1, "bank3")
+        add_hidden(both, 6, 1, 0)
+        empty(4, 1, "slot6", nc.vector.tensor_copy)
+        open_piece((0,), 7, 1, "bank2")
+        open_piece((1,), 7, 1, "bank5")
+        quantise_h(7, 1)
+        add_hidden((0,), 7, 1, 0)
+        add_hidden((1,), 7, 1, 0)
+        empty(6, 1, "staged6", nc.scalar.copy)
+        empty(5, 1, "slot7", nc.vector.tensor_copy)
+        staged = keep.tile([P, 2, CHUNK], F32, name="staged7", align_bytes=64)
+        nc.vector.tensor_copy(out=staged[:, 0, :], in_=banks[(7, 0)][:, 0, :])
+        nc.scalar.copy(out=staged[:, 1, :], in_=banks[(7, 1)][:, 0, :])
+        store(7, 1, staged)

@@ -19,13 +19,13 @@ P = 128
 PACK = 4
 CHUNK = 128
 SCALAR_SHARE = 52
-WARM_PASSES = 4
+WARM_PASSES = 6
 WARM_WIDTH = 256
 
 
-def load_scale_rows(queues, plane, rows):
-    for r in range(4):
-        queues[r % len(queues)].dma_start(out=plane[r:P:32, :].bitcast(I32), in_=rows[r:16:4, :].bitcast(I32))
+def load_scale_rows(queue, plane, rows, which):
+    for r in which:
+        queue.dma_start(out=plane[r:P:32, :].bitcast(I32), in_=rows[r:16:4, :].bitcast(I32))
 
 
 def tile_picked_lora_gelu_p_kernel(
@@ -40,6 +40,7 @@ def tile_picked_lora_gelu_p_kernel(
         xs_table = keep.tile([P, T], U8, name="xs_table", align_bytes=64)
         xw_table = keep.tile([P, T], I32, name="xw_table", align_bytes=64)
         warm = keep.tile([P, 16], F32, name="warm")
+        zeros = keep.tile([P, PACK * WARM_WIDTH], BF16, name="zeros", align_bytes=64)
         w2_raw = keep.tile([P, PACK, H], F32, name="w2_raw", tag="raw", align_bytes=64)
         w1_plane = keep.tile([P, N], U8, name="w1_plane", align_bytes=64)
         x_plane = keep.tile([P, S], U8, name="x_plane", align_bytes=64)
@@ -47,27 +48,40 @@ def tile_picked_lora_gelu_p_kernel(
         nc.vector.memset(xs_table[:].bitcast(I32), 0)
         nc.vector.memset(warm[:, 0:1], 0.0)
         nc.vector.memset(w1_plane[:].bitcast(I32), 0)
-        nc.vector.memset(x_plane[:].bitcast(I32), 0)
         w3_plane = keep.tile([P, N], U8, name="w3_plane", align_bytes=64)
-        nc.gpsimd.memset(w3_plane[:].bitcast(I32), 0)
-        w1_codes = keep.tile([P, 2 * N], U8, name="w1_codes", align_bytes=64)
-        w3_codes = keep.tile([P, 2 * N], U8, name="w3_codes", align_bytes=64)
+        nc.vector.memset(w3_plane[:].bitcast(I32), 0)
+        nc.vector.memset(x_plane[:].bitcast(I32), 0)
+        nc.vector.memset(zeros[:].bitcast(I32), 0)
+        zero_codes = keep.tile([P, WARM_WIDTH], U32, name="zero_codes", align_bytes=64)
+        zero_plane = keep.tile([P, WARM_WIDTH], U8, name="zero_plane", align_bytes=64)
+        nc.vector.quantize_mx(out=zero_codes[:].bitcast(FP8X4), scales=zero_plane[:], in_=zeros[:])
 
         nc.sync.dma_start(offsets[:], offs)
         w2_rows = w2.rearrange("(p j) c -> p j c", j=PACK)
+        w1_codes = keep.tile([P, 2 * N], U8, name="w1_codes", align_bytes=64)
+        w3_codes = keep.tile([P, 2 * N], U8, name="w3_codes", align_bytes=64)
         nc.sync.dma_start(out=w1_codes[:].bitcast(I32), in_=w1_words[0].bitcast(I32))
         nc.sync.dma_start(out=w3_codes[:].bitcast(I32), in_=w3_words[0].bitcast(I32))
         nc.sync.dma_start(out=xs_table[0:P:8, :].bitcast(I32), in_=x_scales[0].bitcast(I32))
         nc.sync.dma_start(out=w2_raw[:], in_=w2_rows)
+        load_scale_rows(nc.sync, w3_plane, w3_scales[0], (0, 1))
         nc.sync.dma_start(out=xw_table[:], in_=x_words[0].rearrange("p n t -> p (n t)").bitcast(I32))
+        load_scale_rows(nc.sync, w3_plane, w3_scales[0], (2,))
         nc.scalar.activation(out=warm[:, 8:9], in_=warm[:, 0:1], func=GELU)
-        load_scale_rows([nc.scalar], w1_plane, w1_scales[0])
-        load_scale_rows([nc.gpsimd], w3_plane, w3_scales[0])
+        load_scale_rows(nc.scalar, w1_plane, w1_scales[0], range(4))
 
         picked = keep.tile([P, S], U8, name="picked", align_bytes=64)
         nc.vector.tensor_copy(picked[:], xs_table[:].indirect(offsets[:]))
         for r in range(4):
             nc.sync.dma_start(out=x_plane[r:P:32, :].bitcast(I32), in_=picked[8 * r : P : 32, :].bitcast(I32))
+        load_scale_rows(nc.sync, w3_plane, w3_scales[0], (3,))
+
+        warm_bank = psum.tile([P, WARM_WIDTH], F32, name="warm_bank", tag="bank5")
+        for i in range(WARM_PASSES):
+            nc.tensor.matmul_mx(
+                out=warm_bank[:], lhsT=zero_codes[:, 0:P].bitcast(FP8X4), lhsT_scale=zero_plane[:, 0:P],
+                rhs=zero_codes[:].bitcast(FP8X4), rhs_scale=picked[:, 0:WARM_WIDTH], start=True, stop=True,
+            )
 
         w2_codes = keep.tile([P, PACK * P], U32, name="w2_codes", align_bytes=64)
         w2_plane = keep.tile([P, PACK * P], U8, name="w2_plane", align_bytes=64)
@@ -79,13 +93,6 @@ def tile_picked_lora_gelu_p_kernel(
         nc.vector.quantize_mx(
             out=w2_codes[:].bitcast(FP8X4), scales=w2_plane[:], in_=grouped[:].rearrange("p t m j -> p (t m j)")
         )
-
-        warm_bank = psum.tile([P, WARM_WIDTH], F32, name="warm_bank", tag="bank5")
-        for i in range(WARM_PASSES):
-            nc.tensor.matmul_mx(
-                out=warm_bank[:], lhsT=w2_codes[:, 0:P].bitcast(FP8X4), lhsT_scale=w2_plane[:, 0:P],
-                rhs=w2_codes[:, 0:WARM_WIDTH].bitcast(FP8X4), rhs_scale=w2_plane[:, 0:WARM_WIDTH], start=True, stop=True,
-            )
 
 
         x_codes = {}
@@ -187,10 +194,10 @@ def tile_picked_lora_gelu_p_kernel(
         add_hidden(both, 0, 2, 0)
         add_hidden(both, 0, 2, 1)
         hidden(5, "bank1")
-        empty(0, 2, "staged0", nc.vector.tensor_copy)
         open_piece(both, 2, 2, "bank2")
         hidden(6, "bank3")
         quantise_h(2, 2)
+        empty(0, 2, "slot2", nc.vector.tensor_copy)
         add_hidden(both, 2, 2, 0)
         add_hidden(both, 2, 2, 1)
         hidden(7, "bank0")

@@ -19,8 +19,8 @@ P = 128
 PACK = 4
 CHUNK = 128
 SCALAR_SHARE = 52
-WARM_PASSES = 6
-WARM_WIDTH = 256
+WARM_PASSES = 4
+WARM_WIDTH = 512
 
 
 def load_scale_rows(queue, plane, rows, which):
@@ -39,19 +39,18 @@ def tile_picked_lora_gelu_p_kernel(
         offsets = keep.tile([P, S // 16], U16, name="offsets")
         xs_table = keep.tile([P, T], U8, name="xs_table", align_bytes=64)
         xw_table = keep.tile([P, T], I32, name="xw_table", align_bytes=64)
-        warm = keep.tile([P, 16], F32, name="warm")
+        warm = keep.tile([P, 1], F32, name="warm")
         zeros = keep.tile([P, PACK * WARM_WIDTH], BF16, name="zeros", align_bytes=64)
         w2_raw = keep.tile([P, PACK, H], F32, name="w2_raw", tag="raw", align_bytes=64)
         w1_plane = keep.tile([P, N], U8, name="w1_plane", align_bytes=64)
         x_plane = keep.tile([P, S], U8, name="x_plane", align_bytes=64)
 
         nc.vector.memset(xs_table[:].bitcast(I32), 0)
-        nc.vector.memset(warm[:, 0:1], 0.0)
+        nc.vector.memset(zeros[:].bitcast(I32), 0)
         nc.vector.memset(w1_plane[:].bitcast(I32), 0)
         w3_plane = keep.tile([P, N], U8, name="w3_plane", align_bytes=64)
         nc.vector.memset(w3_plane[:].bitcast(I32), 0)
         nc.vector.memset(x_plane[:].bitcast(I32), 0)
-        nc.vector.memset(zeros[:].bitcast(I32), 0)
         zero_codes = keep.tile([P, WARM_WIDTH], U32, name="zero_codes", align_bytes=64)
         zero_plane = keep.tile([P, WARM_WIDTH], U8, name="zero_plane", align_bytes=64)
         nc.vector.quantize_mx(out=zero_codes[:].bitcast(FP8X4), scales=zero_plane[:], in_=zeros[:])
@@ -67,7 +66,7 @@ def tile_picked_lora_gelu_p_kernel(
         load_scale_rows(nc.sync, w3_plane, w3_scales[0], (0, 1))
         nc.sync.dma_start(out=xw_table[:], in_=x_words[0].rearrange("p n t -> p (n t)").bitcast(I32))
         load_scale_rows(nc.sync, w3_plane, w3_scales[0], (2,))
-        nc.scalar.activation(out=warm[:, 8:9], in_=warm[:, 0:1], func=GELU)
+        nc.scalar.activation(out=warm[:], in_=zeros[:, 0:1], func=GELU)
         load_scale_rows(nc.scalar, w1_plane, w1_scales[0], range(4))
 
         picked = keep.tile([P, S], U8, name="picked", align_bytes=64)

@@ -18,7 +18,7 @@ GELU = mybir.ActivationFunctionType.Gelu_apprx_tanh
 P = 128
 PACK = 4
 CHUNK = 128
-SCALAR_SHARE = 52
+SCALAR_SHARE = 60
 WARM_PASSES = 4
 WARM_WIDTH = 512
 
@@ -216,9 +216,9 @@ def tile_picked_lora_gelu_p_kernel(
         quantise_h(7, 1)
         add_hidden((0,), 7, 1, 0)
         add_hidden((1,), 7, 1, 0)
-        empty(6, 1, "staged6", nc.scalar.copy)
+        staged = keep.tile([P, 2, 2 * CHUNK], F32, name="staged6", align_bytes=64)
+        nc.scalar.copy(out=staged[:, :, :CHUNK], in_=banks[(6, 0)][:])
         empty(5, 1, "slot7", nc.vector.tensor_copy)
-        staged = keep.tile([P, 2, CHUNK], F32, name="staged7", align_bytes=64)
-        nc.vector.tensor_copy(out=staged[:, 0, :], in_=banks[(7, 0)][:, 0, :])
-        nc.scalar.copy(out=staged[:, 1, :], in_=banks[(7, 1)][:, 0, :])
-        store(7, 1, staged)
+        nc.vector.tensor_copy(out=staged[:, 0, CHUNK:], in_=banks[(7, 0)][:, 0, :])
+        nc.scalar.copy(out=staged[:, 1, CHUNK:], in_=banks[(7, 1)][:, 0, :])
+        store(6, 2, staged)

@@ -18,7 +18,8 @@ GELU = mybir.ActivationFunctionType.Gelu_apprx_tanh
 P = 128
 PACK = 4
 CHUNK = 128
-SCALAR_SHARE = 60
+CHUNKS = S // CHUNK
+SCALAR_SHARE = 68
 WARM_PASSES = 4
 WARM_WIDTH = 512
 
@@ -37,62 +38,62 @@ def tile_picked_lora_gelu_p_kernel(
         psum = ctx.enter_context(tc.psum_pool(name="psum", bufs=1))
 
         offsets = keep.tile([P, S // 16], U16, name="offsets")
-        xs_table = keep.tile([P, T], U8, name="xs_table", align_bytes=64)
+        xs_table = keep.tile([P, T], U8, name="xs_table", tag="table", align_bytes=64)
         xw_table = keep.tile([P, T], I32, name="xw_table", align_bytes=64)
         warm = keep.tile([P, 1], F32, name="warm")
-        zeros = keep.tile([P, PACK * WARM_WIDTH], BF16, name="zeros", align_bytes=64)
-        w2_raw = keep.tile([P, PACK, H], F32, name="w2_raw", tag="raw", align_bytes=64)
+        zeros = keep.tile([P, P], BF16, name="zeros", align_bytes=64)
+        w2_raw = keep.tile([P, PACK * H], F32, name="w2_raw", align_bytes=64)
         w1_plane = keep.tile([P, N], U8, name="w1_plane", align_bytes=64)
+        w3_plane = keep.tile([P, N], U8, name="w3_plane", align_bytes=64)
         x_plane = keep.tile([P, S], U8, name="x_plane", align_bytes=64)
 
         nc.vector.memset(xs_table[:].bitcast(I32), 0)
-        nc.vector.memset(zeros[:].bitcast(I32), 0)
         nc.vector.memset(w1_plane[:].bitcast(I32), 0)
-        w3_plane = keep.tile([P, N], U8, name="w3_plane", align_bytes=64)
         nc.vector.memset(w3_plane[:].bitcast(I32), 0)
-        nc.vector.memset(x_plane[:].bitcast(I32), 0)
+        nc.vector.memset(zeros[:].bitcast(I32), 0)
         zero_codes = keep.tile([P, WARM_WIDTH], U32, name="zero_codes", align_bytes=64)
-        zero_plane = keep.tile([P, WARM_WIDTH], U8, name="zero_plane", align_bytes=64)
-        nc.vector.quantize_mx(out=zero_codes[:].bitcast(FP8X4), scales=zero_plane[:], in_=zeros[:])
+        zero_plane = keep.tile([P, P // PACK], U8, name="zero_plane", align_bytes=64)
+        nc.vector.memset(zero_codes[:], 0)
+        nc.vector.memset(x_plane[:].bitcast(I32), 0)
+        nc.vector.quantize_mx(out=zero_codes[:, : P // PACK].bitcast(FP8X4), scales=zero_plane[:], in_=zeros[:])
 
         nc.sync.dma_start(offsets[:], offs)
-        w2_rows = w2.rearrange("(p j) c -> p j c", j=PACK)
-        w1_codes = keep.tile([P, 2 * N], U8, name="w1_codes", align_bytes=64)
-        w3_codes = keep.tile([P, 2 * N], U8, name="w3_codes", align_bytes=64)
-        nc.sync.dma_start(out=w1_codes[:].bitcast(I32), in_=w1_words[0].bitcast(I32))
-        nc.sync.dma_start(out=w3_codes[:].bitcast(I32), in_=w3_words[0].bitcast(I32))
+        w2_rows = w2.rearrange("(p j) c -> p (j c)", j=PACK)
+        nc.sync.dma_start(out=w2_raw[:, :H], in_=w2_rows[:, :H])
         nc.sync.dma_start(out=xs_table[0:P:8, :].bitcast(I32), in_=x_scales[0].bitcast(I32))
-        nc.sync.dma_start(out=w2_raw[:], in_=w2_rows)
+        nc.sync.dma_start(out=w2_raw[:, H:], in_=w2_rows[:, H:])
         load_scale_rows(nc.sync, w3_plane, w3_scales[0], (0, 1))
         nc.sync.dma_start(out=xw_table[:], in_=x_words[0].rearrange("p n t -> p (n t)").bitcast(I32))
-        load_scale_rows(nc.sync, w3_plane, w3_scales[0], (2,))
+        w1_codes = keep.tile([P, 2 * N], U8, name="w1_codes", align_bytes=64)
+        nc.sync.dma_start(out=w1_codes[:].bitcast(I32), in_=w1_words[0].bitcast(I32))
         nc.scalar.activation(out=warm[:], in_=zeros[:, 0:1], func=GELU)
         load_scale_rows(nc.scalar, w1_plane, w1_scales[0], range(4))
+        load_scale_rows(nc.scalar, w3_plane, w3_scales[0], (2, 3))
 
         picked = keep.tile([P, S], U8, name="picked", align_bytes=64)
         nc.vector.tensor_copy(picked[:], xs_table[:].indirect(offsets[:]))
         for r in range(4):
             nc.sync.dma_start(out=x_plane[r:P:32, :].bitcast(I32), in_=picked[8 * r : P : 32, :].bitcast(I32))
-        load_scale_rows(nc.sync, w3_plane, w3_scales[0], (3,))
+        w3_codes = keep.tile([P, 2 * N], U8, name="w3_codes", tag="table", align_bytes=64)
+        nc.sync.dma_start(out=w3_codes[:].bitcast(I32), in_=w3_words[0].bitcast(I32))
 
-        warm_bank = psum.tile([P, WARM_WIDTH], F32, name="warm_bank", tag="bank5")
+        warm_bank = psum.tile([P, WARM_WIDTH], F32, name="warm_bank", tag="out4")
         for i in range(WARM_PASSES):
             nc.tensor.matmul_mx(
-                out=warm_bank[:], lhsT=zero_codes[:, 0:P].bitcast(FP8X4), lhsT_scale=zero_plane[:, 0:P],
+                out=warm_bank[:], lhsT=zero_codes[:, 0:P].bitcast(FP8X4), lhsT_scale=w1_plane[:, 0:P],
                 rhs=zero_codes[:].bitcast(FP8X4), rhs_scale=picked[:, 0:WARM_WIDTH], start=True, stop=True,
             )
 
         w2_codes = keep.tile([P, PACK * P], U32, name="w2_codes", align_bytes=64)
         w2_plane = keep.tile([P, PACK * P], U8, name="w2_plane", align_bytes=64)
         grouped = keep.tile([P, PACK, P, PACK], BF16, name="w2_grouped", align_bytes=64)
-        src = w2_raw[:].rearrange("p j (m t) -> p m j t", t=PACK)
+        src = w2_raw[:].rearrange("p (j m t) -> p m j t", j=PACK, t=PACK)
         dst = grouped[:].rearrange("p t m j -> p m j t")
         nc.scalar.copy(out=dst[:, :SCALAR_SHARE], in_=src[:, :SCALAR_SHARE])
         nc.vector.tensor_copy(out=dst[:, SCALAR_SHARE:], in_=src[:, SCALAR_SHARE:])
         nc.vector.quantize_mx(
             out=w2_codes[:].bitcast(FP8X4), scales=w2_plane[:], in_=grouped[:].rearrange("p t m j -> p (t m j)")
         )
-
 
         x_codes = {}
 
@@ -121,14 +122,10 @@ def tile_picked_lora_gelu_p_kernel(
 
         h_codes = keep.tile([P, S], U32, name="h_codes", align_bytes=64)
         h_plane = keep.tile([P, S], U8, name="h_plane", align_bytes=64)
-        h_tiles = {}
-        for first, count in ((0, 2), (2, 2), (4, 1), (5, 1), (6, 1), (7, 1)):
-            tile = keep.tile([P, count * CHUNK * PACK], BF16, name=f"h_vals{first}", tag=f"slot{first}", align_bytes=64)
-            for i in range(count):
-                h_tiles[first + i] = (tile, i)
+        h_vals = [keep.tile([P, CHUNK * PACK], BF16, name=f"h_vals{c}", tag=f"slot{c}", align_bytes=64) for c in range(CHUNKS)]
 
-        def hidden(c, tag):
-            bank = psum.tile([P, PACK, CHUNK], F32, name=f"hbank{c}", tag=tag)
+        def hidden(c):
+            bank = psum.tile([P, PACK, CHUNK], F32, name=f"hbank{c}", tag=f"hid{c % 3}")
             rhs = x_operand(c)
             for t in range(PACK):
                 nc.tensor.matmul_mx(
@@ -140,17 +137,12 @@ def tile_picked_lora_gelu_p_kernel(
                     start=True,
                     stop=True,
                 )
-            tile, i = h_tiles[c]
-            dst = tile[:, i * CHUNK * PACK : (i + 1) * CHUNK * PACK].rearrange("p (n t) -> p n t", t=PACK)
+            dst = h_vals[c][:].rearrange("p (n t) -> p n t", t=PACK)
             nc.scalar.activation(out=dst, in_=bank[:].rearrange("p t n -> p n t"), func=GELU)
 
-        def quantise_h(first, count):
-            lo, width = first * CHUNK, count * CHUNK
-            nc.vector.quantize_mx(
-                out=h_codes[:, lo : lo + width].bitcast(FP8X4),
-                scales=h_plane[:, lo : lo + width],
-                in_=h_tiles[first][0][:],
-            )
+        def quantise_h(c):
+            cols = slice(c * CHUNK, (c + 1) * CHUNK)
+            nc.vector.quantize_mx(out=h_codes[:, cols].bitcast(FP8X4), scales=h_plane[:, cols], in_=h_vals[c][:])
 
         def h_operand(c):
             return h_codes[:, c * CHUNK : (c + 1) * CHUNK].bitcast(FP8X4), h_plane[:, c * CHUNK : (c + 1) * CHUNK]
@@ -158,67 +150,67 @@ def tile_picked_lora_gelu_p_kernel(
         out_rows = out.rearrange("(m p) s -> p m s", p=P)
         banks = {}
 
-        def open_piece(ms, first, count, tag):
-            bank = psum.tile([P, len(ms), count * CHUNK], F32, name=f"obank_{first}_{ms[0]}", tag=tag)
-            banks[(first, ms[0])] = bank
-            for i in range(count):
-                for k, m in enumerate(ms):
-                    weight_pass(
-                        bank[:, k, i * CHUNK : (i + 1) * CHUNK], w1_codes, w1_plane, m,
-                        x_operand(first + i), i == 0 and k == 0, False,
-                    )
-
-        def add_hidden(ms, first, count, i):
-            bank = banks[(first, ms[0])]
+        def open_bank(c, tag, ms=(0, 1)):
+            bank = psum.tile([P, len(ms), CHUNK], F32, name=f"obank_{c}_{ms[0]}", tag=tag)
+            banks[(c, ms[0])] = bank
             for k, m in enumerate(ms):
-                weight_pass(
-                    bank[:, k, i * CHUNK : (i + 1) * CHUNK], w3_codes, w3_plane, m,
-                    h_operand(first + i), False, i == count - 1 and k == len(ms) - 1,
-                )
+                weight_pass(bank[:, k, :], w1_codes, w1_plane, m, x_operand(c), k == 0, False)
 
-        def store(first, count, staged):
-            nc.sync.dma_start(out=out_rows[:, :, first * CHUNK : (first + count) * CHUNK], in_=staged[:])
+        def close_bank(c, ms=(0, 1)):
+            bank = banks[(c, ms[0])]
+            for k, m in enumerate(ms):
+                weight_pass(bank[:, k, :], w3_codes, w3_plane, m, h_operand(c), False, k == len(ms) - 1)
 
-        def empty(first, count, tag, copy):
-            staged = keep.tile([P, 2, count * CHUNK], F32, name=f"staged{first}", tag=tag, align_bytes=64)
-            copy(out=staged[:], in_=banks[(first, 0)][:])
-            store(first, count, staged)
+        def store(c, staged):
+            nc.sync.dma_start(out=out_rows[:, :, c * CHUNK : (c + 1) * CHUNK], in_=staged[:])
 
-        both = (0, 1)
-        for c in range(4):
-            hidden(c, f"bank{c}")
-        open_piece(both, 0, 2, "bank4")
-        hidden(4, "bank0")
-        quantise_h(0, 2)
-        add_hidden(both, 0, 2, 0)
-        add_hidden(both, 0, 2, 1)
-        hidden(5, "bank1")
-        open_piece(both, 2, 2, "bank2")
-        hidden(6, "bank3")
-        quantise_h(2, 2)
-        empty(0, 2, "slot2", nc.vector.tensor_copy)
-        add_hidden(both, 2, 2, 0)
-        add_hidden(both, 2, 2, 1)
-        hidden(7, "bank0")
-        quantise_h(4, 1)
-        open_piece(both, 4, 1, "bank4")
-        add_hidden(both, 4, 1, 0)
-        quantise_h(5, 1)
-        empty(2, 2, "slot5", nc.vector.tensor_copy)
-        open_piece(both, 5, 1, "bank1")
-        add_hidden(both, 5, 1, 0)
-        quantise_h(6, 1)
-        open_piece(both, 6, 1, "bank3")
-        add_hidden(both, 6, 1, 0)
-        empty(4, 1, "slot6", nc.vector.tensor_copy)
-        open_piece((0,), 7, 1, "bank2")
-        open_piece((1,), 7, 1, "bank5")
-        quantise_h(7, 1)
-        add_hidden((0,), 7, 1, 0)
-        add_hidden((1,), 7, 1, 0)
-        staged = keep.tile([P, 2, 2 * CHUNK], F32, name="staged6", align_bytes=64)
-        nc.scalar.copy(out=staged[:, :, :CHUNK], in_=banks[(6, 0)][:])
-        empty(5, 1, "slot7", nc.vector.tensor_copy)
-        nc.vector.tensor_copy(out=staged[:, 0, CHUNK:], in_=banks[(7, 0)][:, 0, :])
-        nc.scalar.copy(out=staged[:, 1, CHUNK:], in_=banks[(7, 1)][:, 0, :])
-        store(6, 2, staged)
+        def empty(c, tag, copy):
+            staged = keep.tile([P, 2, CHUNK], F32, name=f"staged{c}", tag=tag, align_bytes=64)
+            copy(out=staged[:], in_=banks[(c, 0)][:])
+            store(c, staged)
+
+        hidden(0)
+        hidden(1)
+        open_bank(0, "out0")
+        open_bank(1, "out1")
+        hidden(2)
+        hidden(3)
+        open_bank(2, "out2")
+        open_bank(3, "out3")
+        quantise_h(0)
+        quantise_h(1)
+        hidden(4)
+        close_bank(0)
+        quantise_h(2)
+        hidden(5)
+        close_bank(1)
+        empty(0, "staged0", nc.vector.tensor_copy)
+        open_bank(4, "out4")
+        quantise_h(3)
+        hidden(6)
+        close_bank(2)
+        empty(1, "staged1", nc.vector.tensor_copy)
+        quantise_h(4)
+        close_bank(3)
+        hidden(7)
+        empty(2, "staged2", nc.vector.tensor_copy)
+        open_bank(5, "out0")
+        close_bank(4)
+        quantise_h(5)
+        empty(3, "staged3", nc.vector.tensor_copy)
+        open_bank(6, "out1")
+        close_bank(5)
+        open_bank(7, "out2", (0,))
+        open_bank(7, "hid2", (1,))
+        quantise_h(6)
+        empty(4, "staged4", nc.vector.tensor_copy)
+        close_bank(6)
+        quantise_h(7)
+        close_bank(7, (0,))
+        close_bank(7, (1,))
+        empty(6, "staged6", nc.scalar.copy)
+        empty(5, "staged5", nc.vector.tensor_copy)
+        staged = keep.tile([P, 2, CHUNK], F32, name="staged7", align_bytes=64)
+        nc.vector.tensor_copy(out=staged[:, 0, :], in_=banks[(7, 0)][:, 0, :])
+        nc.scalar.copy(out=staged[:, 1, :], in_=banks[(7, 1)][:, 0, :])
+        store(7, staged)

@@ -19,7 +19,7 @@ P = 128
 PACK = 4
 CHUNK = 128
 CHUNKS = S // CHUNK
-SCALAR_SHARE = 68
+SCALAR_SHARE = 76
 WARM_PASSES = 4
 WARM_WIDTH = 512
 
@@ -38,7 +38,7 @@ def tile_picked_lora_gelu_p_kernel(
         psum = ctx.enter_context(tc.psum_pool(name="psum", bufs=1))
 
         offsets = keep.tile([P, S // 16], U16, name="offsets")
-        xs_table = keep.tile([P, T], U8, name="xs_table", tag="table", align_bytes=64)
+        xs_table = keep.tile([P, T], U8, name="xs_table", align_bytes=64)
         xw_table = keep.tile([P, T], I32, name="xw_table", align_bytes=64)
         warm = keep.tile([P, 1], F32, name="warm")
         zeros = keep.tile([P, P], BF16, name="zeros", align_bytes=64)
@@ -47,40 +47,40 @@ def tile_picked_lora_gelu_p_kernel(
         w3_plane = keep.tile([P, N], U8, name="w3_plane", align_bytes=64)
         x_plane = keep.tile([P, S], U8, name="x_plane", align_bytes=64)
 
+        nc.vector.memset(zeros[:].bitcast(I32), 0)
         nc.vector.memset(xs_table[:].bitcast(I32), 0)
         nc.vector.memset(w1_plane[:].bitcast(I32), 0)
         nc.vector.memset(w3_plane[:].bitcast(I32), 0)
-        nc.vector.memset(zeros[:].bitcast(I32), 0)
         zero_codes = keep.tile([P, WARM_WIDTH], U32, name="zero_codes", align_bytes=64)
         zero_plane = keep.tile([P, P // PACK], U8, name="zero_plane", align_bytes=64)
         nc.vector.memset(zero_codes[:], 0)
         nc.vector.memset(x_plane[:].bitcast(I32), 0)
         nc.vector.quantize_mx(out=zero_codes[:, : P // PACK].bitcast(FP8X4), scales=zero_plane[:], in_=zeros[:])
 
-        nc.sync.dma_start(offsets[:], offs)
         w2_rows = w2.rearrange("(p j) c -> p (j c)", j=PACK)
         nc.sync.dma_start(out=w2_raw[:, :H], in_=w2_rows[:, :H])
+        nc.sync.dma_start(offsets[:], offs)
         nc.sync.dma_start(out=xs_table[0:P:8, :].bitcast(I32), in_=x_scales[0].bitcast(I32))
         nc.sync.dma_start(out=w2_raw[:, H:], in_=w2_rows[:, H:])
-        load_scale_rows(nc.sync, w3_plane, w3_scales[0], (0, 1))
+        load_scale_rows(nc.sync, w3_plane, w3_scales[0], (0,))
         nc.sync.dma_start(out=xw_table[:], in_=x_words[0].rearrange("p n t -> p (n t)").bitcast(I32))
-        w1_codes = keep.tile([P, 2 * N], U8, name="w1_codes", align_bytes=64)
-        nc.sync.dma_start(out=w1_codes[:].bitcast(I32), in_=w1_words[0].bitcast(I32))
+        load_scale_rows(nc.sync, w3_plane, w3_scales[0], (1, 2, 3))
         nc.scalar.activation(out=warm[:], in_=zeros[:, 0:1], func=GELU)
         load_scale_rows(nc.scalar, w1_plane, w1_scales[0], range(4))
-        load_scale_rows(nc.scalar, w3_plane, w3_scales[0], (2, 3))
 
         picked = keep.tile([P, S], U8, name="picked", align_bytes=64)
         nc.vector.tensor_copy(picked[:], xs_table[:].indirect(offsets[:]))
         for r in range(4):
             nc.sync.dma_start(out=x_plane[r:P:32, :].bitcast(I32), in_=picked[8 * r : P : 32, :].bitcast(I32))
-        w3_codes = keep.tile([P, 2 * N], U8, name="w3_codes", tag="table", align_bytes=64)
+        w1_codes = keep.tile([P, 2 * N], U8, name="w1_codes", align_bytes=64)
+        nc.sync.dma_start(out=w1_codes[:].bitcast(I32), in_=w1_words[0].bitcast(I32))
+        w3_codes = keep.tile([P, 2 * N], U8, name="w3_codes", align_bytes=64)
         nc.sync.dma_start(out=w3_codes[:].bitcast(I32), in_=w3_words[0].bitcast(I32))
 
         warm_bank = psum.tile([P, WARM_WIDTH], F32, name="warm_bank", tag="out4")
         for i in range(WARM_PASSES):
             nc.tensor.matmul_mx(
-                out=warm_bank[:], lhsT=zero_codes[:, 0:P].bitcast(FP8X4), lhsT_scale=w1_plane[:, 0:P],
+                out=warm_bank[:], lhsT=zero_codes[:, 0:P].bitcast(FP8X4), lhsT_scale=picked[:, 0:P],
                 rhs=zero_codes[:].bitcast(FP8X4), rhs_scale=picked[:, 0:WARM_WIDTH], start=True, stop=True,
             )
 
@@ -171,9 +171,9 @@ def tile_picked_lora_gelu_p_kernel(
 
         hidden(0)
         hidden(1)
+        hidden(2)
         open_bank(0, "out0")
         open_bank(1, "out1")
-        hidden(2)
         hidden(3)
         open_bank(2, "out2")
         open_bank(3, "out3")
@@ -208,8 +208,8 @@ def tile_picked_lora_gelu_p_kernel(
         quantise_h(7)
         close_bank(7, (0,))
         close_bank(7, (1,))
+        empty(5, "staged5", nc.scalar.copy)
         empty(6, "staged6", nc.scalar.copy)
-        empty(5, "staged5", nc.vector.tensor_copy)
         staged = keep.tile([P, 2, CHUNK], F32, name="staged7", align_bytes=64)
         nc.vector.tensor_copy(out=staged[:, 0, :], in_=banks[(7, 0)][:, 0, :])
         nc.scalar.copy(out=staged[:, 1, :], in_=banks[(7, 1)][:, 0, :])

@@ -19,9 +19,8 @@ P = 128
 PACK = 4
 CHUNK = 128
 CHUNKS = S // CHUNK
-SCALAR_SHARE = 76
-WARM_PASSES = 4
-WARM_WIDTH = 512
+SCALAR_SHARE = 64
+WORD_GATHERS = (128, 128, 256, 512)
 
 
 def load_scale_rows(queue, plane, rows, which):
@@ -40,49 +39,33 @@ def tile_picked_lora_gelu_p_kernel(
         offsets = keep.tile([P, S // 16], U16, name="offsets")
         xs_table = keep.tile([P, T], U8, name="xs_table", align_bytes=64)
         xw_table = keep.tile([P, T], I32, name="xw_table", align_bytes=64)
-        warm = keep.tile([P, 1], F32, name="warm")
-        zeros = keep.tile([P, P], BF16, name="zeros", align_bytes=64)
         w2_raw = keep.tile([P, PACK * H], F32, name="w2_raw", align_bytes=64)
-        w1_plane = keep.tile([P, N], U8, name="w1_plane", align_bytes=64)
-        w3_plane = keep.tile([P, N], U8, name="w3_plane", align_bytes=64)
-        x_plane = keep.tile([P, S], U8, name="x_plane", align_bytes=64)
+        w_planes = keep.tile([P, 2 * N], U8, name="w_planes", align_bytes=64)
+        w1_plane, w3_plane = w_planes[:, :N], w_planes[:, N:]
+        w1_codes = keep.tile([P, 2 * N], U8, name="w1_codes", align_bytes=64)
+        w3_codes = keep.tile([P, 2 * N], U8, name="w3_codes", align_bytes=64)
 
-        nc.vector.memset(zeros[:].bitcast(I32), 0)
         nc.vector.memset(xs_table[:].bitcast(I32), 0)
-        nc.vector.memset(w1_plane[:].bitcast(I32), 0)
-        nc.vector.memset(w3_plane[:].bitcast(I32), 0)
-        zero_codes = keep.tile([P, WARM_WIDTH], U32, name="zero_codes", align_bytes=64)
-        zero_plane = keep.tile([P, P // PACK], U8, name="zero_plane", align_bytes=64)
-        nc.vector.memset(zero_codes[:], 0)
-        nc.vector.memset(x_plane[:].bitcast(I32), 0)
-        nc.vector.quantize_mx(out=zero_codes[:, : P // PACK].bitcast(FP8X4), scales=zero_plane[:], in_=zeros[:])
+        nc.vector.memset(w_planes[:].bitcast(I32), 0)
 
         w2_rows = w2.rearrange("(p j) c -> p (j c)", j=PACK)
-        nc.sync.dma_start(out=w2_raw[:, :H], in_=w2_rows[:, :H])
         nc.sync.dma_start(offsets[:], offs)
-        nc.sync.dma_start(out=xs_table[0:P:8, :].bitcast(I32), in_=x_scales[0].bitcast(I32))
+        nc.sync.dma_start(out=w2_raw[:, :H], in_=w2_rows[:, :H])
+        load_scale_rows(nc.scalar, xs_table, x_scales[0], (2, 3))
+        load_scale_rows(nc.sync, xs_table, x_scales[0], (0, 1))
         nc.sync.dma_start(out=w2_raw[:, H:], in_=w2_rows[:, H:])
-        load_scale_rows(nc.sync, w3_plane, w3_scales[0], (0,))
         nc.sync.dma_start(out=xw_table[:], in_=x_words[0].rearrange("p n t -> p (n t)").bitcast(I32))
-        load_scale_rows(nc.sync, w3_plane, w3_scales[0], (1, 2, 3))
-        nc.scalar.activation(out=warm[:], in_=zeros[:, 0:1], func=GELU)
+
+        warm = keep.tile([P, 1], F32, name="warm")
+        nc.scalar.activation(out=warm[:], in_=w_planes[:, 0:4].bitcast(F32), func=GELU)
         load_scale_rows(nc.scalar, w1_plane, w1_scales[0], range(4))
-
-        picked = keep.tile([P, S], U8, name="picked", align_bytes=64)
-        nc.vector.tensor_copy(picked[:], xs_table[:].indirect(offsets[:]))
-        for r in range(4):
-            nc.sync.dma_start(out=x_plane[r:P:32, :].bitcast(I32), in_=picked[8 * r : P : 32, :].bitcast(I32))
-        w1_codes = keep.tile([P, 2 * N], U8, name="w1_codes", align_bytes=64)
+        load_scale_rows(nc.scalar, w3_plane, w3_scales[0], (0, 1))
         nc.sync.dma_start(out=w1_codes[:].bitcast(I32), in_=w1_words[0].bitcast(I32))
-        w3_codes = keep.tile([P, 2 * N], U8, name="w3_codes", align_bytes=64)
         nc.sync.dma_start(out=w3_codes[:].bitcast(I32), in_=w3_words[0].bitcast(I32))
+        load_scale_rows(nc.sync, w3_plane, w3_scales[0], (2, 3))
 
-        warm_bank = psum.tile([P, WARM_WIDTH], F32, name="warm_bank", tag="out4")
-        for i in range(WARM_PASSES):
-            nc.tensor.matmul_mx(
-                out=warm_bank[:], lhsT=zero_codes[:, 0:P].bitcast(FP8X4), lhsT_scale=picked[:, 0:P],
-                rhs=zero_codes[:].bitcast(FP8X4), rhs_scale=picked[:, 0:WARM_WIDTH], start=True, stop=True,
-            )
+        x_plane = keep.tile([P, S], U8, name="x_plane", align_bytes=64)
+        nc.vector.tensor_copy(x_plane[:], xs_table[:].indirect(offsets[:]))
 
         w2_codes = keep.tile([P, PACK * P], U32, name="w2_codes", align_bytes=64)
         w2_plane = keep.tile([P, PACK * P], U8, name="w2_plane", align_bytes=64)
@@ -95,122 +78,112 @@ def tile_picked_lora_gelu_p_kernel(
             out=w2_codes[:].bitcast(FP8X4), scales=w2_plane[:], in_=grouped[:].rearrange("p t m j -> p (t m j)")
         )
 
-        x_codes = {}
-
-        def gather_words(lo, width):
-            codes = keep.tile([P, width], U32, name=f"x_codes{lo}", align_bytes=64)
-            nc.vector.tensor_copy(codes[:], xw_table[:].bitcast(U32).indirect(offsets[:, lo // 16 : (lo + width) // 16]))
-            for c in range(0, width, CHUNK):
-                x_codes[(lo + c) // CHUNK] = codes[:, c : c + CHUNK]
-
-        for lo, width in ((0, 256), (256, 256), (512, 512)):
-            gather_words(lo, width)
-
-        def x_operand(c):
-            return x_codes[c].bitcast(FP8X4), x_plane[:, c * CHUNK : (c + 1) * CHUNK]
-
-        def weight_pass(dst, codes, plane, m, rhs, start, stop):
-            nc.tensor.matmul_mx(
-                out=dst,
-                lhsT=codes[:, 2 * P * m : 2 * P * (m + 1)].bitcast(FP4X4),
-                lhsT_scale=plane[:, P * m : P * (m + 1)],
-                rhs=rhs[0],
-                rhs_scale=rhs[1],
-                start=start,
-                stop=stop,
+        x_codes = keep.tile([P, S], U32, name="x_codes", align_bytes=64)
+        lo = 0
+        for width in WORD_GATHERS:
+            nc.vector.tensor_copy(
+                x_codes[:, lo : lo + width], xw_table[:].bitcast(U32).indirect(offsets[:, lo // 16 : (lo + width) // 16])
             )
+            lo = lo + width
 
         h_codes = keep.tile([P, S], U32, name="h_codes", align_bytes=64)
         h_plane = keep.tile([P, S], U8, name="h_plane", align_bytes=64)
-        h_vals = [keep.tile([P, CHUNK * PACK], BF16, name=f"h_vals{c}", tag=f"slot{c}", align_bytes=64) for c in range(CHUNKS)]
+        h_vals = keep.tile([P, (S - CHUNK) * PACK], BF16, name="h_vals", align_bytes=64)
+        h_last = keep.tile([P, CHUNK * PACK], BF16, name="h_last", tag="last", align_bytes=64)
+
+        def h_values(c, count=1):
+            if c == CHUNKS - 1:
+                return h_last[:]
+            return h_vals[:, c * CHUNK * PACK : (c + count) * CHUNK * PACK]
+
+        def tokens(c, count=1):
+            return slice(c * CHUNK, (c + count) * CHUNK)
 
         def hidden(c):
-            bank = psum.tile([P, PACK, CHUNK], F32, name=f"hbank{c}", tag=f"hid{c % 3}")
-            rhs = x_operand(c)
+            bank = psum.tile([P, PACK, CHUNK], F32, name=f"hbank{c}", tag=f"bank{c}")
             for t in range(PACK):
                 nc.tensor.matmul_mx(
                     out=bank[:, t, :],
                     lhsT=w2_codes[:, t * P : (t + 1) * P].bitcast(FP8X4),
                     lhsT_scale=w2_plane[:, t * P : (t + 1) * P],
-                    rhs=rhs[0],
-                    rhs_scale=rhs[1],
+                    rhs=x_codes[:, tokens(c)].bitcast(FP8X4),
+                    rhs_scale=x_plane[:, tokens(c)],
                     start=True,
                     stop=True,
                 )
-            dst = h_vals[c][:].rearrange("p (n t) -> p n t", t=PACK)
+            dst = h_values(c).rearrange("p (n t) -> p n t", t=PACK)
             nc.scalar.activation(out=dst, in_=bank[:].rearrange("p t n -> p n t"), func=GELU)
 
-        def quantise_h(c):
-            cols = slice(c * CHUNK, (c + 1) * CHUNK)
-            nc.vector.quantize_mx(out=h_codes[:, cols].bitcast(FP8X4), scales=h_plane[:, cols], in_=h_vals[c][:])
+        def quantise_h(c, count=1):
+            nc.vector.quantize_mx(
+                out=h_codes[:, tokens(c, count)].bitcast(FP8X4),
+                scales=h_plane[:, tokens(c, count)],
+                in_=h_values(c, count),
+            )
 
-        def h_operand(c):
-            return h_codes[:, c * CHUNK : (c + 1) * CHUNK].bitcast(FP8X4), h_plane[:, c * CHUNK : (c + 1) * CHUNK]
+        def weight_pass(dst, codes, plane, m, rhs_codes, rhs_plane, start, stop):
+            nc.tensor.matmul_mx(
+                out=dst,
+                lhsT=codes[:, 2 * P * m : 2 * P * (m + 1)].bitcast(FP4X4),
+                lhsT_scale=plane[:, P * m : P * (m + 1)],
+                rhs=rhs_codes.bitcast(FP8X4),
+                rhs_scale=rhs_plane,
+                start=start,
+                stop=stop,
+            )
 
         out_rows = out.rearrange("(m p) s -> p m s", p=P)
         banks = {}
 
-        def open_bank(c, tag, ms=(0, 1)):
-            bank = psum.tile([P, len(ms), CHUNK], F32, name=f"obank_{c}_{ms[0]}", tag=tag)
+        def open_bank(c, count, tag, ms=(0, 1)):
+            bank = psum.tile([P, len(ms), count * CHUNK], F32, name=f"obank_{c}_{ms[0]}", tag=tag)
             banks[(c, ms[0])] = bank
+            cols = tokens(c, count)
             for k, m in enumerate(ms):
-                weight_pass(bank[:, k, :], w1_codes, w1_plane, m, x_operand(c), k == 0, False)
+                weight_pass(bank[:, k, :], w1_codes, w1_plane, m, x_codes[:, cols], x_plane[:, cols], k == 0, False)
 
-        def close_bank(c, ms=(0, 1)):
+        def close_bank(c, count, ms=(0, 1)):
             bank = banks[(c, ms[0])]
+            cols = tokens(c, count)
             for k, m in enumerate(ms):
-                weight_pass(bank[:, k, :], w3_codes, w3_plane, m, h_operand(c), False, k == len(ms) - 1)
+                weight_pass(bank[:, k, :], w3_codes, w3_plane, m, h_codes[:, cols], h_plane[:, cols], False, k == len(ms) - 1)
 
-        def store(c, staged):
-            nc.sync.dma_start(out=out_rows[:, :, c * CHUNK : (c + 1) * CHUNK], in_=staged[:])
-
-        def empty(c, tag, copy):
-            staged = keep.tile([P, 2, CHUNK], F32, name=f"staged{c}", tag=tag, align_bytes=64)
+        def empty(c, count, copy, tag=None):
+            staged = keep.tile([P, 2, count * CHUNK], F32, name=f"staged{c}", tag=tag or f"staged{c}", align_bytes=64)
             copy(out=staged[:], in_=banks[(c, 0)][:])
-            store(c, staged)
+            nc.sync.dma_start(out=out_rows[:, :, tokens(c, count)], in_=staged[:])
 
-        hidden(0)
-        hidden(1)
-        hidden(2)
-        open_bank(0, "out0")
-        open_bank(1, "out1")
-        hidden(3)
-        open_bank(2, "out2")
-        open_bank(3, "out3")
-        quantise_h(0)
-        quantise_h(1)
-        hidden(4)
-        close_bank(0)
-        quantise_h(2)
+        for c in range(5):
+            hidden(c)
+        quantise_h(0, 2)
+        open_bank(0, 2, "bank0")
+        close_bank(0, 2)
         hidden(5)
-        close_bank(1)
-        empty(0, "staged0", nc.vector.tensor_copy)
-        open_bank(4, "out4")
-        quantise_h(3)
+        quantise_h(2, 2)
+        open_bank(2, 2, "bank1")
+        empty(0, 2, nc.vector.tensor_copy)
         hidden(6)
-        close_bank(2)
-        empty(1, "staged1", nc.vector.tensor_copy)
+        close_bank(2, 2)
         quantise_h(4)
-        close_bank(3)
         hidden(7)
-        empty(2, "staged2", nc.vector.tensor_copy)
-        open_bank(5, "out0")
-        close_bank(4)
+        empty(2, 2, nc.vector.tensor_copy)
         quantise_h(5)
-        empty(3, "staged3", nc.vector.tensor_copy)
-        open_bank(6, "out1")
-        close_bank(5)
-        open_bank(7, "out2", (0,))
-        open_bank(7, "hid2", (1,))
+        open_bank(4, 1, "bank2")
+        close_bank(4, 1)
+        open_bank(5, 1, "bank3")
+        close_bank(5, 1)
         quantise_h(6)
-        empty(4, "staged4", nc.vector.tensor_copy)
-        close_bank(6)
+        open_bank(6, 1, "bank4")
+        open_bank(7, 1, "bank5", (0,))
+        open_bank(7, 1, "bank6", (1,))
+        close_bank(6, 1)
         quantise_h(7)
-        close_bank(7, (0,))
-        close_bank(7, (1,))
-        empty(5, "staged5", nc.scalar.copy)
-        empty(6, "staged6", nc.scalar.copy)
+        close_bank(7, 1, (0,))
+        close_bank(7, 1, (1,))
+        empty(4, 1, nc.scalar.copy)
+        empty(5, 1, nc.vector.tensor_copy, "last")
+        empty(6, 1, nc.scalar.copy)
         staged = keep.tile([P, 2, CHUNK], F32, name="staged7", align_bytes=64)
         nc.vector.tensor_copy(out=staged[:, 0, :], in_=banks[(7, 0)][:, 0, :])
         nc.scalar.copy(out=staged[:, 1, :], in_=banks[(7, 1)][:, 0, :])
-        store(7, staged)
+        nc.sync.dma_start(out=out_rows[:, :, tokens(7)], in_=staged[:])

@@ -19,13 +19,17 @@ P = 128
 PACK = 4
 CHUNK = 128
 CHUNKS = S // CHUNK
-SCALAR_SHARE = 64
+SCALAR_SHARE = 60
 WORD_GATHERS = (128, 128, 256, 512)
 
 
-def load_scale_rows(queue, plane, rows, which):
-    for r in which:
-        queue.dma_start(out=plane[r:P:32, :].bitcast(I32), in_=rows[r:16:4, :].bitcast(I32))
+def load_spread(queue, table, rows):
+    queue.dma_start(out=table[0:P:8, :].bitcast(I32), in_=rows.bitcast(I32))
+
+
+def move_rows(queue, plane, table):
+    for r in range(4):
+        queue.dma_start(out=plane[r:P:32, :].bitcast(I32), in_=table[8 * r : P : 32, :].bitcast(I32))
 
 
 def tile_picked_lora_gelu_p_kernel(
@@ -39,33 +43,32 @@ def tile_picked_lora_gelu_p_kernel(
         offsets = keep.tile([P, S // 16], U16, name="offsets")
         xs_table = keep.tile([P, T], U8, name="xs_table", align_bytes=64)
         xw_table = keep.tile([P, T], I32, name="xw_table", align_bytes=64)
-        w2_raw = keep.tile([P, PACK * H], F32, name="w2_raw", align_bytes=64)
-        w_planes = keep.tile([P, 2 * N], U8, name="w_planes", align_bytes=64)
-        w1_plane, w3_plane = w_planes[:, :N], w_planes[:, N:]
+        w2_raw = keep.tile([P, PACK * H], F32, name="w2_raw", tag="raw", align_bytes=64)
+        w_spread = keep.tile([P, 2 * N], U8, name="w_spread", align_bytes=64)
         w1_codes = keep.tile([P, 2 * N], U8, name="w1_codes", align_bytes=64)
         w3_codes = keep.tile([P, 2 * N], U8, name="w3_codes", align_bytes=64)
+        x_plane = keep.tile([P, S], U8, name="x_plane", align_bytes=64)
 
         nc.vector.memset(xs_table[:].bitcast(I32), 0)
-        nc.vector.memset(w_planes[:].bitcast(I32), 0)
+        nc.vector.memset(x_plane[:].bitcast(I32), 0)
 
         w2_rows = w2.rearrange("(p j) c -> p (j c)", j=PACK)
-        nc.sync.dma_start(offsets[:], offs)
         nc.sync.dma_start(out=w2_raw[:, :H], in_=w2_rows[:, :H])
-        load_scale_rows(nc.scalar, xs_table, x_scales[0], (2, 3))
-        load_scale_rows(nc.sync, xs_table, x_scales[0], (0, 1))
+        nc.sync.dma_start(offsets[:], offs)
+        load_spread(nc.sync, xs_table[:], x_scales[0])
         nc.sync.dma_start(out=w2_raw[:, H:], in_=w2_rows[:, H:])
         nc.sync.dma_start(out=xw_table[:], in_=x_words[0].rearrange("p n t -> p (n t)").bitcast(I32))
+        load_spread(nc.scalar, w_spread[:, :N], w1_scales[0])
+        load_spread(nc.scalar, w_spread[:, N:], w3_scales[0])
 
         warm = keep.tile([P, 1], F32, name="warm")
-        nc.scalar.activation(out=warm[:], in_=w_planes[:, 0:4].bitcast(F32), func=GELU)
-        load_scale_rows(nc.scalar, w1_plane, w1_scales[0], range(4))
-        load_scale_rows(nc.scalar, w3_plane, w3_scales[0], (0, 1))
+        nc.scalar.activation(out=warm[:], in_=w2_raw[:, 0:1], func=GELU)
+
+        picked = keep.tile([P, S], U8, name="picked", align_bytes=64)
+        nc.vector.tensor_copy(picked[:], xs_table[:].indirect(offsets[:]))
+        move_rows(nc.sync, x_plane[:], picked[:])
         nc.sync.dma_start(out=w1_codes[:].bitcast(I32), in_=w1_words[0].bitcast(I32))
         nc.sync.dma_start(out=w3_codes[:].bitcast(I32), in_=w3_words[0].bitcast(I32))
-        load_scale_rows(nc.sync, w3_plane, w3_scales[0], (2, 3))
-
-        x_plane = keep.tile([P, S], U8, name="x_plane", align_bytes=64)
-        nc.vector.tensor_copy(x_plane[:], xs_table[:].indirect(offsets[:]))
 
         w2_codes = keep.tile([P, PACK * P], U32, name="w2_codes", align_bytes=64)
         w2_plane = keep.tile([P, PACK * P], U8, name="w2_plane", align_bytes=64)
@@ -74,6 +77,9 @@ def tile_picked_lora_gelu_p_kernel(
         dst = grouped[:].rearrange("p t m j -> p m j t")
         nc.scalar.copy(out=dst[:, :SCALAR_SHARE], in_=src[:, :SCALAR_SHARE])
         nc.vector.tensor_copy(out=dst[:, SCALAR_SHARE:], in_=src[:, SCALAR_SHARE:])
+        w_planes = keep.tile([P, 2 * N], U8, name="w_planes", tag="raw", align_bytes=64)
+        w1_plane, w3_plane = w_planes[:, :N], w_planes[:, N:]
+        move_rows(nc.scalar, w_planes[:], w_spread[:])
         nc.vector.quantize_mx(
             out=w2_codes[:].bitcast(FP8X4), scales=w2_plane[:], in_=grouped[:].rearrange("p t m j -> p (t m j)")
         )

@@ -19,7 +19,8 @@ P = 128
 PACK = 4
 CHUNK = 128
 CHUNKS = S // CHUNK
-SCALAR_SHARE = 60
+LEAD = 256
+SCALAR_SHARE = 54
 WORD_GATHERS = (128, 128, 256, 512)
 
 
@@ -53,13 +54,13 @@ def tile_picked_lora_gelu_p_kernel(
         nc.vector.memset(x_plane[:].bitcast(I32), 0)
 
         w2_rows = w2.rearrange("(p j) c -> p (j c)", j=PACK)
-        nc.sync.dma_start(out=w2_raw[:, :H], in_=w2_rows[:, :H])
+        nc.sync.dma_start(out=w2_raw[:, :LEAD], in_=w2_rows[:, :LEAD])
         nc.sync.dma_start(offsets[:], offs)
         load_spread(nc.sync, xs_table[:], x_scales[0])
-        nc.sync.dma_start(out=w2_raw[:, H:], in_=w2_rows[:, H:])
+        nc.sync.dma_start(out=w2_raw[:, LEAD:], in_=w2_rows[:, LEAD:])
         nc.sync.dma_start(out=xw_table[:], in_=x_words[0].rearrange("p n t -> p (n t)").bitcast(I32))
-        load_spread(nc.scalar, w_spread[:, :N], w1_scales[0])
-        load_spread(nc.scalar, w_spread[:, N:], w3_scales[0])
+        load_spread(nc.sync, w_spread[:, :N], w1_scales[0])
+        load_spread(nc.sync, w_spread[:, N:], w3_scales[0])
 
         warm = keep.tile([P, 1], F32, name="warm")
         nc.scalar.activation(out=warm[:], in_=w2_raw[:, 0:1], func=GELU)

@@ -160,6 +160,12 @@ def tile_picked_lora_gelu_p_kernel(
             copy(out=staged[:], in_=banks[(c, 0)][:])
             nc.sync.dma_start(out=out_rows[:, :, tokens(c, count)], in_=staged[:])
 
+        def empty_by_rows(c, count):
+            for m in range(2):
+                staged = keep.tile([P, count * CHUNK], F32, name=f"staged{c}_{m}", align_bytes=64)
+                nc.vector.tensor_copy(out=staged[:], in_=banks[(c, 0)][:, m, :])
+                nc.sync.dma_start(out=out_rows[:, m, tokens(c, count)], in_=staged[:])
+
         for c in range(5):
             hidden(c)
         quantise_h(0, 2)
@@ -173,7 +179,7 @@ def tile_picked_lora_gelu_p_kernel(
         close_bank(2, 2)
         quantise_h(4)
         hidden(7)
-        empty(2, 2, nc.vector.tensor_copy)
+        empty_by_rows(2, 2)
         quantise_h(5)
         open_bank(4, 1, "bank2")
         close_bank(4, 1)
@@ -189,8 +195,8 @@ def tile_picked_lora_gelu_p_kernel(
         close_bank(7, 1, (1,))
         empty(4, 1, nc.scalar.copy)
         empty(5, 1, nc.vector.tensor_copy, "last")
-        empty(6, 1, nc.scalar.copy)
-        staged = keep.tile([P, 2, CHUNK], F32, name="staged7", align_bytes=64)
-        nc.vector.tensor_copy(out=staged[:, 0, :], in_=banks[(7, 0)][:, 0, :])
-        nc.scalar.copy(out=staged[:, 1, :], in_=banks[(7, 1)][:, 0, :])
-        nc.sync.dma_start(out=out_rows[:, :, tokens(7)], in_=staged[:])
+        staged = keep.tile([P, 2, 2 * CHUNK], F32, name="staged_end", align_bytes=64)
+        nc.scalar.copy(out=staged[:, :, :CHUNK], in_=banks[(6, 0)][:])
+        nc.vector.tensor_copy(out=staged[:, 0, CHUNK:], in_=banks[(7, 0)][:, 0, :])
+        nc.scalar.copy(out=staged[:, 1, CHUNK:], in_=banks[(7, 1)][:, 0, :])
+        nc.sync.dma_start(out=out_rows[:, :, tokens(6, 2)], in_=staged[:])

@@ -19,13 +19,19 @@ P = 128
 PACK = 4
 CHUNK = 128
 CHUNKS = S // CHUNK
-LEAD = 256
-SCALAR_SHARE = 54
+SCALE_ROWS = 16
+FIRST_ROW = P - SCALE_ROWS
+SCALAR_SHARE = 48
 WORD_GATHERS = (128, 128, 256, 512)
 
 
 def load_spread(queue, table, rows):
     queue.dma_start(out=table[0:P:8, :].bitcast(I32), in_=rows.bitcast(I32))
+
+
+def move_top_rows(queue, plane, table):
+    for r in range(4):
+        queue.dma_start(out=plane[r:P:32, :].bitcast(I32), in_=table[FIRST_ROW + r : P : 4, :].bitcast(I32))
 
 
 def move_rows(queue, plane, table):
@@ -50,24 +56,23 @@ def tile_picked_lora_gelu_p_kernel(
         w3_codes = keep.tile([P, 2 * N], U8, name="w3_codes", align_bytes=64)
         x_plane = keep.tile([P, S], U8, name="x_plane", align_bytes=64)
 
-        nc.vector.memset(xs_table[:].bitcast(I32), 0)
+        nc.vector.memset(xs_table[:FIRST_ROW, :].bitcast(I32), 0)
         nc.vector.memset(x_plane[:].bitcast(I32), 0)
 
-        w2_rows = w2.rearrange("(p j) c -> p (j c)", j=PACK)
-        nc.sync.dma_start(out=w2_raw[:, :LEAD], in_=w2_rows[:, :LEAD])
+        nc.sync.dma_start(out=xs_table[FIRST_ROW:, :].bitcast(I32), in_=x_scales[0].bitcast(I32))
         nc.sync.dma_start(offsets[:], offs)
-        load_spread(nc.sync, xs_table[:], x_scales[0])
-        nc.sync.dma_start(out=w2_raw[:, LEAD:], in_=w2_rows[:, LEAD:])
+        nc.sync.dma_start(out=w2_raw[:], in_=w2.rearrange("(p j) c -> p (j c)", j=PACK))
         nc.sync.dma_start(out=xw_table[:], in_=x_words[0].rearrange("p n t -> p (n t)").bitcast(I32))
         load_spread(nc.sync, w_spread[:, :N], w1_scales[0])
         load_spread(nc.sync, w_spread[:, N:], w3_scales[0])
 
         warm = keep.tile([P, 1], F32, name="warm")
-        nc.scalar.activation(out=warm[:], in_=w2_raw[:, 0:1], func=GELU)
+        nc.gpsimd.memset(warm[:], 0.0)
+        nc.scalar.activation(out=warm[:], in_=warm[:], func=GELU)
 
         picked = keep.tile([P, S], U8, name="picked", align_bytes=64)
         nc.vector.tensor_copy(picked[:], xs_table[:].indirect(offsets[:]))
-        move_rows(nc.sync, x_plane[:], picked[:])
+        move_top_rows(nc.sync, x_plane[:], picked[:])
         nc.sync.dma_start(out=w1_codes[:].bitcast(I32), in_=w1_words[0].bitcast(I32))
         nc.sync.dma_start(out=w3_codes[:].bitcast(I32), in_=w3_words[0].bitcast(I32))
 

@@ -21,7 +21,8 @@ CHUNK = 128
 CHUNKS = S // CHUNK
 SCALE_ROWS = 16
 FIRST_ROW = P - SCALE_ROWS
-SCALAR_SHARE = 48
+LEAD = 256
+SCALAR_SHARE = 52
 WORD_GATHERS = (128, 128, 256, 512)
 
 
@@ -59,16 +60,17 @@ def tile_picked_lora_gelu_p_kernel(
         nc.vector.memset(xs_table[:FIRST_ROW, :].bitcast(I32), 0)
         nc.vector.memset(x_plane[:].bitcast(I32), 0)
 
+        w2_rows = w2.rearrange("(p j) c -> p (j c)", j=PACK)
+        nc.sync.dma_start(out=w2_raw[:, :LEAD], in_=w2_rows[:, :LEAD])
         nc.sync.dma_start(out=xs_table[FIRST_ROW:, :].bitcast(I32), in_=x_scales[0].bitcast(I32))
         nc.sync.dma_start(offsets[:], offs)
-        nc.sync.dma_start(out=w2_raw[:], in_=w2.rearrange("(p j) c -> p (j c)", j=PACK))
+        nc.sync.dma_start(out=w2_raw[:, LEAD:], in_=w2_rows[:, LEAD:])
         nc.sync.dma_start(out=xw_table[:], in_=x_words[0].rearrange("p n t -> p (n t)").bitcast(I32))
         load_spread(nc.sync, w_spread[:, :N], w1_scales[0])
         load_spread(nc.sync, w_spread[:, N:], w3_scales[0])
 
         warm = keep.tile([P, 1], F32, name="warm")
-        nc.gpsimd.memset(warm[:], 0.0)
-        nc.scalar.activation(out=warm[:], in_=warm[:], func=GELU)
+        nc.scalar.activation(out=warm[:], in_=w2_raw[:, 0:1], func=GELU)
 
         picked = keep.tile([P, S], U8, name="picked", align_bytes=64)
         nc.vector.tensor_copy(picked[:], xs_table[:].indirect(offsets[:]))

@@ -167,11 +167,10 @@ def tile_picked_lora_gelu_p_kernel(
             copy(out=staged[:], in_=banks[(c, 0)][:])
             nc.sync.dma_start(out=out_rows[:, :, tokens(c, count)], in_=staged[:])
 
-        def empty_by_rows(c, count):
-            for m in range(2):
-                staged = keep.tile([P, count * CHUNK], F32, name=f"staged{c}_{m}", align_bytes=64)
-                nc.vector.tensor_copy(out=staged[:], in_=banks[(c, 0)][:, m, :])
-                nc.sync.dma_start(out=out_rows[:, m, tokens(c, count)], in_=staged[:])
+        def empty_rows(c, count, m, copy):
+            staged = keep.tile([P, count * CHUNK], F32, name=f"staged{c}_{m}", align_bytes=64)
+            copy(out=staged[:], in_=banks[(c, 0)][:, m, :])
+            nc.sync.dma_start(out=out_rows[:, m, tokens(c, count)], in_=staged[:])
 
         for c in range(5):
             hidden(c)
@@ -186,7 +185,7 @@ def tile_picked_lora_gelu_p_kernel(
         close_bank(2, 2)
         quantise_h(4)
         hidden(7)
-        empty_by_rows(2, 2)
+        empty_rows(2, 2, 0, nc.vector.tensor_copy)
         quantise_h(5)
         open_bank(4, 1, "bank2")
         close_bank(4, 1)
@@ -200,6 +199,7 @@ def tile_picked_lora_gelu_p_kernel(
         quantise_h(7)
         close_bank(7, 1, (0,))
         close_bank(7, 1, (1,))
+        empty_rows(2, 2, 1, nc.scalar.copy)
         empty(4, 1, nc.scalar.copy)
         empty(5, 1, nc.vector.tensor_copy, "last")
         staged = keep.tile([P, 2, 2 * CHUNK], F32, name="staged_end", align_bytes=64)

from contextlib import ExitStack

import concourse.mybir as mybir

K, T, S, H, N = 512, 2048, 1024, 512, 256
FLOPS = 2 * K * H * S + 2 * K * N * S + 2 * H * N * S

F32 = mybir.dt.float32
BF16 = mybir.dt.bfloat16
I32 = mybir.dt.int32
U32 = mybir.dt.uint32
U16 = mybir.dt.uint16
U8 = mybir.dt.uint8
FP8X4 = mybir.dt.float8_e4m3fn_x4
FP4X4 = mybir.dt.float4_e2m1fn_x4
GELU = mybir.ActivationFunctionType.Gelu_apprx_tanh

P = 128
PACK = 4
CHUNK = 128
CHUNKS = S // CHUNK
SCALE_ROWS = 16
FIRST_ROW = P - SCALE_ROWS
LEAD = 256
SCALAR_SHARE = 52
WORD_GATHERS = (128, 128, 256, 512)


def load_spread(queue, table, rows):
    queue.dma_start(out=table[0:P:8, :].bitcast(I32), in_=rows.bitcast(I32))


def move_top_rows(queue, plane, table):
    for r in range(4):
        queue.dma_start(out=plane[r:P:32, :].bitcast(I32), in_=table[FIRST_ROW + r : P : 4, :].bitcast(I32))


def move_rows(queue, plane, table):
    for r in range(4):
        queue.dma_start(out=plane[r:P:32, :].bitcast(I32), in_=table[8 * r : P : 32, :].bitcast(I32))


def tile_picked_lora_gelu_p_kernel(
    tc, x_words, x_scales, w1_words, w1_scales, w2, w3_words, w3_scales, offs, out
):
    nc = tc.nc
    with ExitStack() as ctx:
        keep = ctx.enter_context(tc.tile_pool(name="keep", bufs=1))
        psum = ctx.enter_context(tc.psum_pool(name="psum", bufs=1))

        offsets = keep.tile([P, S // 16], U16, name="offsets")
        xs_table = keep.tile([P, T], U8, name="xs_table", align_bytes=64)
        xw_table = keep.tile([P, T], I32, name="xw_table", align_bytes=64)
        w2_raw = keep.tile([P, PACK * H], F32, name="w2_raw", tag="raw", align_bytes=64)
        w_spread = keep.tile([P, 2 * N], U8, name="w_spread", align_bytes=64)
        w1_codes = keep.tile([P, 2 * N], U8, name="w1_codes", align_bytes=64)
        w3_codes = keep.tile([P, 2 * N], U8, name="w3_codes", align_bytes=64)
        x_plane = keep.tile([P, S], U8, name="x_plane", align_bytes=64)

        nc.vector.memset(xs_table[:FIRST_ROW, :].bitcast(I32), 0)
        nc.vector.memset(x_plane[:].bitcast(I32), 0)

        w2_rows = w2.rearrange("(p j) c -> p (j c)", j=PACK)
        nc.sync.dma_start(out=w2_raw[:, :LEAD], in_=w2_rows[:, :LEAD])
        nc.sync.dma_start(out=xs_table[FIRST_ROW:, :].bitcast(I32), in_=x_scales[0].bitcast(I32))
        nc.sync.dma_start(offsets[:], offs)
        nc.sync.dma_start(out=w2_raw[:, LEAD:], in_=w2_rows[:, LEAD:])
        nc.sync.dma_start(out=xw_table[:], in_=x_words[0].rearrange("p n t -> p (n t)").bitcast(I32))
        load_spread(nc.sync, w_spread[:, :N], w1_scales[0])
        load_spread(nc.sync, w_spread[:, N:], w3_scales[0])

        warm = keep.tile([P, 1], F32, name="warm")
        nc.scalar.activation(out=warm[:], in_=w2_raw[:, 0:1], func=GELU)

        picked = keep.tile([P, S], U8, name="picked", align_bytes=64)
        nc.vector.tensor_copy(picked[:], xs_table[:].indirect(offsets[:]))
        move_top_rows(nc.sync, x_plane[:], picked[:])
        nc.sync.dma_start(out=w1_codes[:].bitcast(I32), in_=w1_words[0].bitcast(I32))
        nc.sync.dma_start(out=w3_codes[:].bitcast(I32), in_=w3_words[0].bitcast(I32))

        w2_codes = keep.tile([P, PACK * P], U32, name="w2_codes", align_bytes=64)
        w2_plane = keep.tile([P, PACK * P], U8, name="w2_plane", align_bytes=64)
        grouped = keep.tile([P, PACK, P, PACK], BF16, name="w2_grouped", align_bytes=64)
        src = w2_raw[:].rearrange("p (j m t) -> p m j t", j=PACK, t=PACK)
        dst = grouped[:].rearrange("p t m j -> p m j t")
        nc.scalar.copy(out=dst[:, :SCALAR_SHARE], in_=src[:, :SCALAR_SHARE])
        nc.vector.tensor_copy(out=dst[:, SCALAR_SHARE:], in_=src[:, SCALAR_SHARE:])
        w_planes = keep.tile([P, 2 * N], U8, name="w_planes", tag="raw", align_bytes=64)
        w1_plane, w3_plane = w_planes[:, :N], w_planes[:, N:]
        move_rows(nc.scalar, w_planes[:], w_spread[:])
        nc.vector.quantize_mx(
            out=w2_codes[:].bitcast(FP8X4), scales=w2_plane[:], in_=grouped[:].rearrange("p t m j -> p (t m j)")
        )

        x_codes = keep.tile([P, S], U32, name="x_codes", align_bytes=64)
        lo = 0
        for width in WORD_GATHERS:
            nc.vector.tensor_copy(
                x_codes[:, lo : lo + width], xw_table[:].bitcast(U32).indirect(offsets[:, lo // 16 : (lo + width) // 16])
            )
            lo = lo + width

        h_codes = keep.tile([P, S], U32, name="h_codes", align_bytes=64)
        h_plane = keep.tile([P, S], U8, name="h_plane", align_bytes=64)
        h_vals = keep.tile([P, (S - CHUNK) * PACK], BF16, name="h_vals", align_bytes=64)
        h_last = keep.tile([P, CHUNK * PACK], BF16, name="h_last", tag="last", align_bytes=64)

        def h_values(c, count=1):
            if c == CHUNKS - 1:
                return h_last[:]
            return h_vals[:, c * CHUNK * PACK : (c + count) * CHUNK * PACK]

        def tokens(c, count=1):
            return slice(c * CHUNK, (c + count) * CHUNK)

        def hidden(c):
            bank = psum.tile([P, PACK, CHUNK], F32, name=f"hbank{c}", tag=f"bank{c}")
            for t in range(PACK):
                nc.tensor.matmul_mx(
                    out=bank[:, t, :],
                    lhsT=w2_codes[:, t * P : (t + 1) * P].bitcast(FP8X4),
                    lhsT_scale=w2_plane[:, t * P : (t + 1) * P],
                    rhs=x_codes[:, tokens(c)].bitcast(FP8X4),
                    rhs_scale=x_plane[:, tokens(c)],
                    start=True,
                    stop=True,
                )
            dst = h_values(c).rearrange("p (n t) -> p n t", t=PACK)
            nc.scalar.activation(out=dst, in_=bank[:].rearrange("p t n -> p n t"), func=GELU)

        def quantise_h(c, count=1):
            nc.vector.quantize_mx(
                out=h_codes[:, tokens(c, count)].bitcast(FP8X4),
                scales=h_plane[:, tokens(c, count)],
                in_=h_values(c, count),
            )

        def weight_pass(dst, codes, plane, m, rhs_codes, rhs_plane, start, stop):
            nc.tensor.matmul_mx(
                out=dst,
                lhsT=codes[:, 2 * P * m : 2 * P * (m + 1)].bitcast(FP4X4),
                lhsT_scale=plane[:, P * m : P * (m + 1)],
                rhs=rhs_codes.bitcast(FP8X4),
                rhs_scale=rhs_plane,
                start=start,
                stop=stop,
            )

        out_rows = out.rearrange("(m p) s -> p m s", p=P)
        banks = {}

        def open_bank(c, count, tag, ms=(0, 1)):
            bank = psum.tile([P, len(ms), count * CHUNK], F32, name=f"obank_{c}_{ms[0]}", tag=tag)
            banks[(c, ms[0])] = bank
            cols = tokens(c, count)
            for k, m in enumerate(ms):
                weight_pass(bank[:, k, :], w1_codes, w1_plane, m, x_codes[:, cols], x_plane[:, cols], k == 0, False)

        def close_bank(c, count, ms=(0, 1)):
            bank = banks[(c, ms[0])]
            cols = tokens(c, count)
            for k, m in enumerate(ms):
                weight_pass(bank[:, k, :], w3_codes, w3_plane, m, h_codes[:, cols], h_plane[:, cols], False, k == len(ms) - 1)

        def empty(c, count, copy, tag=None):
            staged = keep.tile([P, 2, count * CHUNK], F32, name=f"staged{c}", tag=tag or f"staged{c}", align_bytes=64)
            copy(out=staged[:], in_=banks[(c, 0)][:])
            nc.sync.dma_start(out=out_rows[:, :, tokens(c, count)], in_=staged[:])

        def empty_rows(c, count, m, copy):
            staged = keep.tile([P, count * CHUNK], F32, name=f"staged{c}_{m}", align_bytes=64)
            copy(out=staged[:], in_=banks[(c, 0)][:, m, :])
            nc.sync.dma_start(out=out_rows[:, m, tokens(c, count)], in_=staged[:])

        for c in range(5):
            hidden(c)
        quantise_h(0, 2)
        open_bank(0, 2, "bank0")
        close_bank(0, 2)
        hidden(5)
        quantise_h(2, 2)
        open_bank(2, 2, "bank1")
        empty(0, 2, nc.vector.tensor_copy)
        hidden(6)
        close_bank(2, 2)
        quantise_h(4)
        hidden(7)
        empty_rows(2, 2, 0, nc.vector.tensor_copy)
        quantise_h(5)
        open_bank(4, 1, "bank2")
        close_bank(4, 1)
        open_bank(5, 1, "bank3")
        close_bank(5, 1)
        quantise_h(6)
        open_bank(6, 1, "bank4")
        open_bank(7, 1, "bank5", (0,))
        open_bank(7, 1, "bank6", (1,))
        close_bank(6, 1)
        quantise_h(7)
        close_bank(7, 1, (0,))
        close_bank(7, 1, (1,))
        empty_rows(2, 2, 1, nc.scalar.copy)
        empty(4, 1, nc.scalar.copy)
        empty(5, 1, nc.vector.tensor_copy, "last")
        staged = keep.tile([P, 2, 2 * CHUNK], F32, name="staged_end", align_bytes=64)
        nc.scalar.copy(out=staged[:, :, :CHUNK], in_=banks[(6, 0)][:])
        nc.vector.tensor_copy(out=staged[:, 0, CHUNK:], in_=banks[(7, 0)][:, 0, :])
        nc.scalar.copy(out=staged[:, 1, CHUNK:], in_=banks[(7, 1)][:, 0, :])
        nc.sync.dma_start(out=out_rows[:, :, tokens(6, 2)], in_=staged[:])
